import numpy as np
import ml_dtypes


def mxq(x, axis, fmt="e4m3"):
    dtype, down = {"e4m3": (ml_dtypes.float8_e4m3fn, 7), "e5m2": (ml_dtypes.float8_e5m2, 14)}[fmt]
    v = np.moveaxis(np.asarray(x, np.float32).astype(ml_dtypes.bfloat16).astype(np.float64), axis, -1)
    blocks = v.reshape(v.shape[:-1] + (-1, 32))
    amax = np.abs(blocks).max(-1, keepdims=True)
    byte = np.maximum(np.where(amax > 0, np.frexp(amax)[1] - 1 + 127, 0) - down, 1)
    scale = np.exp2(byte - 127.0)
    codes = (blocks / scale).astype(np.float32).astype(dtype).astype(np.float64)
    return np.moveaxis((codes * scale).reshape(v.shape), -1, axis)


WIDE = False


def mx_kscale(k):
    if not WIDE:
        return np.ones(k)
    levels = np.array([10, -10, 5, -5, 0])
    if k % 512:
        return np.exp2(np.random.permutation(np.resize(levels, k // 32))).repeat(32)
    a = np.empty((k // 512, 16))
    for p in range(k // 512):
        a[p, :8] = np.random.permutation(np.resize(levels, 8))
        for g in range(8):
            far = levels[np.abs(levels - a[p, g]) >= 10]
            a[p, g + 8] = far[np.random.randint(len(far))]
    return np.exp2(a.ravel()).repeat(32)


def f64(x):
    return np.asarray(x).astype(np.float64)


def striped(idx):
    return np.tile(idx.reshape(-1, 16).T, (8, 1)).astype(np.uint16)


def unstriped(offs):
    return offs[:16].T.reshape(-1).astype(np.int64)


def pack_weight(w):
    k, n = w.shape
    w = f64(np.asarray(w, np.float32).astype(ml_dtypes.bfloat16)).reshape(k // 32, 32, n)
    amax = np.abs(w).max(1)
    byte = np.clip(np.where(amax > 0, np.frexp(amax)[1] - 1 + 127 - 7, 1), 1, 254)
    scaled = (w * np.exp2(127.0 - byte)[:, None, :]).reshape(k, n).astype(np.float32)
    words = np.ascontiguousarray(scaled.reshape(k // 512, 128, 4, n).transpose(0, 1, 3, 2)).astype(ml_dtypes.float8_e4m3fn).view(np.uint8)
    return words, np.ascontiguousarray(byte.astype(np.uint8).reshape(k // 512, 16, n))


def unpack_weight(words, scales):
    g, p, n, _ = words.shape
    vals = np.ascontiguousarray(words).view(ml_dtypes.float8_e4m3fn).astype(np.float64) * np.repeat(np.exp2(scales.astype(np.float64) - 127.0), 8, axis=1)[..., None]
    return vals.transpose(0, 1, 3, 2).reshape(g * 512, n)


def planes(y):
    n, m = y.shape
    v = y.astype(np.float32).astype(ml_dtypes.bfloat16).astype(np.float64).reshape(n // 32, 32, m)
    top = np.abs(v).max(1)
    byte = np.clip(np.where(top > 0, np.frexp(top)[1] - 1 + 127 - 7, 1), 1, 254)
    codes = (v * np.exp2(127.0 - byte)[:, None, :]).reshape(n, m).astype(np.float32).astype(ml_dtypes.float8_e4m3fn).view(np.uint8)
    words = codes.reshape(n // 512, 128, 4, m).transpose(0, 1, 3, 2)
    return np.ascontiguousarray(words), np.ascontiguousarray(byte.astype(np.uint8).reshape(n // 512, 16, m))


K, T, S, N = 1024, 2048, 512, 512


def setup_inputs():
    n = np.random.standard_normal
    s = mx_kscale(K)[:, None]
    packed_xT = pack_weight(n((K, T)) * s)
    return {
        "x_words": packed_xT[0],
        "x_scales": packed_xT[1],
        "w1": (n((K, N)) / np.sqrt(K) / s).astype(np.float32),
        "offs": striped(np.random.permutation(T)[:S]),
        "style": striped(np.random.permutation(T)[:S]),
    }


def reference(x_words, x_scales, w1, offs, style):
    xq = unpack_weight(x_words, x_scales)[:, unstriped(offs)]
    w1q = mxq(f64(w1), 0, "e4m3")
    y = w1q.T @ xq
    my = y.mean(axis=1, keepdims=True)
    dy = y - my
    x_style = unpack_weight(x_words, x_scales)[:, unstriped(style)]
    z = w1q.T @ x_style
    mz = z.mean(axis=1, keepdims=True)
    dz = z - mz
    qz = (dz) ** 2
    sz = np.sqrt(qz.mean(axis=1, keepdims=True) + 1e-4)
    qy = (dy) ** 2
    sy = np.sqrt(qy.mean(axis=1, keepdims=True) + 1e-4)
    f = sz / sy
    out_0 = dy * f + mz
    return (out_0,) + planes(out_0)

@@ -1,0 +1,216 @@
+from contextlib import ExitStack
+
+import concourse.mybir as mybir
+
+K, T, S, N = 1024, 2048, 512, 512
+EPS = 1e-4
+FLOPS = 2 * 2 * K * N * S
+
+F32 = mybir.dt.float32
+BF16 = mybir.dt.bfloat16
+I32 = mybir.dt.int32
+U32 = mybir.dt.uint32
+U16 = mybir.dt.uint16
+U8 = mybir.dt.uint8
+FP8X4 = mybir.dt.float8_e4m3fn_x4
+ACT = mybir.ActivationFunctionType
+ALU = mybir.AluOpType
+
+P = 128
+PACK = 4
+PASSES = K // (P * PACK)
+QUADS = 4
+
+
+def tile_picked_yadain_none_po_kernel(tc, x_words, x_scales, w1, offs, style, out_0, out_1, out_2):
+    nc = tc.nc
+    with ExitStack() as ctx:
+        keep = ctx.enter_context(tc.tile_pool(name="keep", bufs=1))
+        psum = ctx.enter_context(tc.psum_pool(name="psum", bufs=1))
+
+        def sb(name, shape, dtype):
+            return keep.tile(shape, dtype, name=name, align_bytes=64)
+
+        lists = [sb("offs_sb", [P, S // 16], U16), sb("style_sb", [P, S // 16], U16)]
+        xs = sb("xs", [P, T], U8)
+        xw = [sb("xw%d" % g, [P, T], I32) for g in range(PASSES)]
+        raw = {}
+
+        warm = sb("warm", [P, 1], F32)
+        warm2 = sb("warm2", [P, 1], F32)
+        nc.vector.memset(warm[:], 1.0)
+        nc.vector.memset(xs[:].bitcast(I32), 0)
+        nc.scalar.activation(warm2[:], warm[:], ACT.Sqrt)
+
+        def load_x(g):
+            nc.sync.dma_start(xw[g][:], x_words[g].rearrange("p n t -> p (n t)").bitcast(I32))
+
+        def load_w(g, h):
+            rows = w1[g * P * PACK:(g + 1) * P * PACK, :].rearrange("(p j) c -> p j c", j=PACK)
+            raw[g, h] = sb("raw%d" % h, [P, 2, N], F32)
+            nc.sync.dma_start(raw[g, h][:], rows[:, 2 * h:2 * h + 2, :])
+
+        nc.sync.dma_start(lists[0][:], offs)
+        nc.sync.dma_start(lists[1][:], style)
+        load_x(0)
+        for q in range(QUADS):
+            nc.scalar.dma_start(xs[32 * q:32 * q + 4 * PASSES, :].bitcast(I32), x_scales[:, 4 * q:4 * q + 4, :].bitcast(I32))
+        load_w(0, 0)
+        load_w(0, 1)
+        load_x(1)
+
+        gw = [[sb("gw%d%d" % (g, l), [P, S], I32) for l in range(2)] for g in range(PASSES)]
+        gs = {}
+        wb = [sb("wb%d" % g, [P, PACK, P, PACK], BF16) for g in range(PASSES)]
+        wq = [sb("wq%d" % g, [P, N], U32) for g in range(PASSES)]
+        ws = [sb("ws%d" % g, [P, N], U8) for g in range(PASSES)]
+
+        def gather_words(g, l):
+            nc.vector.tensor_copy(gw[g][l][:].bitcast(U32), xw[g][:].bitcast(U32).indirect(lists[l][:]))
+
+        def gather_scales(l):
+            gs[l] = sb("wb0" if l else "gs0", [P, S], U8)
+            nc.vector.tensor_copy(gs[l][:], xs[:].indirect(lists[l][:]))
+
+        def deal(g, h, m0, m1, on_vector):
+            dst = wb[g][:, :, m0:m1, 2 * h:2 * h + 2].rearrange("p t m j -> p m j t")
+            src = raw[g, h][:, :, PACK * m0:PACK * m1].rearrange("p j (m t) -> p m j t", t=PACK)
+            if on_vector:
+                nc.vector.tensor_copy(dst, src)
+            else:
+                nc.scalar.copy(dst, src)
+
+        def quant_w(g, t0, t1):
+            nc.vector.quantize_mx(
+                out=wq[g][:, P * t0:P * t1].bitcast(FP8X4),
+                scales=ws[g][:, P * t0:P * t1],
+                in_=wb[g][:, t0:t1].rearrange("p t m j -> p (t m j)"),
+            )
+
+        acc = [[psum.tile([P, S], F32, name="acc%d%d" % (l, t)) for t in range(PACK)] for l in range(2)]
+
+        def mm(g, l, t):
+            nc.tensor.matmul_mx(
+                out=acc[l][t][:],
+                lhsT=wq[g][:, P * t:P * (t + 1)].bitcast(FP8X4),
+                lhsT_scale=ws[g][:, P * t:P * (t + 1)],
+                rhs=gw[g][l][:].bitcast(FP8X4),
+                rhs_scale=gs[l][4 * g:P, :],
+                start=(g == 0),
+                stop=(g == PASSES - 1),
+            )
+
+        gather_words(0, 0)
+        gather_words(0, 1)
+        gather_scales(0)
+        deal(0, 0, 0, P, False)
+        load_w(1, 0)
+        deal(0, 1, 0, P, False)
+        load_w(1, 1)
+        quant_w(0, 0, PACK)
+        gather_scales(1)
+        for l in range(2):
+            for t in range(PACK):
+                mm(0, l, t)
+        gather_words(1, 0)
+        gather_words(1, 1)
+        deal(1, 0, 0, P, False)
+        deal(1, 1, 0, 56, True)
+        deal(1, 1, 56, P, False)
+        for t in range(PACK):
+            quant_w(1, t, t + 1)
+        for l, t in ((0, 0), (1, 0), (0, 1), (1, 1), (0, 2), (0, 3), (1, 2), (1, 3)):
+            mm(1, l, t)
+
+        junk = [sb("junk%d" % i, [P, S], BF16) for i in range(4)]
+        negmy = sb("negmy", [P, PACK], F32)
+        m2y = sb("m2y", [P, 2], F32)
+        st = [[sb("st%d%d" % (l, t), [P, 6], F32) for t in range(PACK)] for l in range(2)]
+        mvy = sb("mvy", [P, 2, 2], F32)
+        mvz = [sb("mvz%d" % t, [P, 2], F32) for t in range(PACK)]
+        vye = [sb("vye%d" % u, [P, 2], F32) for u in range(2)]
+        ry = [sb("ry%d" % u, [P, 2], F32) for u in range(2)]
+        er = [sb("er%d" % u, [P, 2], F32) for u in range(2)]
+        f = [sb("f%d" % t, [P, 1], F32) for t in range(PACK)]
+        b = [sb("b%d" % t, [P, 1], F32) for t in range(PACK)]
+        res = sb("res", [P, PACK, S], F32)
+        out_rows = out_0.rearrange("(p t) c -> p t c", t=PACK)
+
+        for t in range(2):
+            nc.scalar.activation(junk[t][:], acc[0][t][:], ACT.Identity, scale=-1.0 / S, accum_out=negmy[:, t:t + 1])
+        for t in range(2):
+            nc.scalar.activation(junk[2 + t][:], acc[0][t][:], ACT.Square, bias=negmy[:, t:t + 1], accum_out=m2y[:, t:t + 1])
+
+        def stats(l, t, mv):
+            nc.vector.bn_stats(st[l][t][:], acc[l][t][:])
+            nc.vector.bn_aggr(mv, st[l][t][:])
+
+        def inverse(u):
+            nc.vector.reciprocal(ry[u][:], vye[u][:])
+            nc.vector.tensor_scalar(er[u][:], ry[u][:], EPS, None, ALU.mult)
+
+        def factors(t):
+            u, i = divmod(t, 2)
+            nc.scalar.activation(f[t][:], mvz[t][:, 1:2], ACT.Sqrt, scale=ry[u][:, i:i + 1], bias=er[u][:, i:i + 1])
+            nc.scalar.activation(b[t][:], f[t][:], ACT.Identity, scale=negmy[:, t:t + 1], bias=mvz[t][:, 0:1])
+
+        def affine(t, c0, c1, on_vector):
+            if on_vector:
+                nc.vector.tensor_scalar(res[:, t, c0:c1], acc[0][t][:, c0:c1], f[t][:], b[t][:], ALU.mult, ALU.add)
+            else:
+                nc.scalar.activation(res[:, t, c0:c1], acc[0][t][:, c0:c1], ACT.Identity, scale=f[t][:], bias=b[t][:])
+
+        def store(t):
+            nc.sync.dma_start(out_rows[:, t, :], res[:, t, :])
+
+        stats(1, 0, mvz[0][:])
+        stats(1, 1, mvz[1][:])
+        stats(0, 2, mvy[:, 0, :])
+        nc.vector.tensor_scalar(vye[0][:], m2y[:], 1.0 / S, EPS, ALU.mult, ALU.add)
+        inverse(0)
+        for t in range(2):
+            factors(t)
+            affine(t, 0, S, False)
+            store(t)
+        stats(0, 3, mvy[:, 1, :])
+        nc.vector.tensor_scalar(vye[1][:], mvy[:, :, 1], EPS, None, ALU.add)
+        nc.vector.tensor_scalar(negmy[:, 2:4], mvy[:, :, 0], -1.0, None, ALU.mult)
+        inverse(1)
+        stats(1, 2, mvz[2][:])
+        factors(2)
+        affine(2, 0, S, False)
+        store(2)
+        stats(1, 3, mvz[3][:])
+        factors(3)
+        affine(3, 0, S, True)
+        store(3)
+
+        rb = sb("rb", [P, S, PACK], BF16)
+        oq = sb("oq", [P, S], U32)
+        osc = sb("osc", [P, S], U8)
+
+        def weave(c0, c1, on_vector):
+            dst = rb[:, c0:c1, :].rearrange("p (c i) t -> p c t i", i=4)
+            src = res[:, :, c0:c1].rearrange("p t (c i) -> p c t i", i=4)
+            if on_vector:
+                nc.vector.tensor_copy(dst, src)
+            else:
+                nc.scalar.copy(dst, src)
+
+        def quant_out(c0, c1):
+            nc.vector.quantize_mx(
+                out=oq[:, c0:c1].bitcast(FP8X4),
+                scales=osc[:, c0:c1],
+                in_=rb[:, c0:c1, :].rearrange("p c t -> p (c t)"),
+            )
+            words = out_1[0].rearrange("p n t -> p (n t)").bitcast(I32)
+            nc.sync.dma_start(words[:, c0:c1], oq[:, c0:c1].bitcast(I32))
+
+        weave(0, 256, True)
+        weave(384, S, False)
+        weave(256, 384, True)
+        quant_out(0, 256)
+        quant_out(256, S)
+        for q in range(QUADS):
+            eng = nc.scalar if q % 2 else nc.sync
+            eng.dma_start(out_2[0, 4 * q:4 * q + 4, :].bitcast(I32), osc[32 * q:32 * q + 4, :].bitcast(I32))

@@ -38,43 +38,42 @@ def tile_picked_yadain_none_po_kernel(tc, x_words, x_scales, w1, offs, style, ou
 
         warm = sb("warm", [P, 1], F32)
         warm2 = sb("warm2", [P, 1], F32)
-        nc.vector.memset(warm[:], 1.0)
         nc.vector.memset(xs[:].bitcast(I32), 0)
-        nc.scalar.activation(warm2[:], warm[:], ACT.Sqrt)
+        nc.vector.memset(warm[:], 1.0)
 
         def load_x(g):
             nc.sync.dma_start(xw[g][:], x_words[g].rearrange("p n t -> p (n t)").bitcast(I32))
 
-        def load_w(g, h):
+        def load_w(g):
             rows = w1[g * P * PACK:(g + 1) * P * PACK, :].rearrange("(p j) c -> p j c", j=PACK)
-            raw[g, h] = sb("raw%d" % h, [P, 2, N], F32)
-            nc.sync.dma_start(raw[g, h][:], rows[:, 2 * h:2 * h + 2, :])
+            raw[g] = sb("raw%d" % g, [P, PACK, N], F32)
+            nc.sync.dma_start(raw[g][:], rows)
 
         nc.sync.dma_start(lists[0][:], offs)
         nc.sync.dma_start(lists[1][:], style)
         load_x(0)
         for q in range(QUADS):
             nc.scalar.dma_start(xs[32 * q:32 * q + 4 * PASSES, :].bitcast(I32), x_scales[:, 4 * q:4 * q + 4, :].bitcast(I32))
-        load_w(0, 0)
-        load_w(0, 1)
+        nc.scalar.activation(warm2[:], warm[:], ACT.Sqrt)
+        load_w(0)
         load_x(1)
+        load_w(1)
 
-        gw = [[sb("gw%d%d" % (g, l), [P, S], I32) for l in range(2)] for g in range(PASSES)]
-        gs = {}
+        gw = {}
+        gs = [sb("gs%d" % l, [P, S], U8) for l in range(2)]
         wb = [sb("wb%d" % g, [P, PACK, P, PACK], BF16) for g in range(PASSES)]
-        wq = [sb("wq%d" % g, [P, N], U32) for g in range(PASSES)]
+        wq = {}
         ws = [sb("ws%d" % g, [P, N], U8) for g in range(PASSES)]
 
         def gather_words(g, l):
-            nc.vector.tensor_copy(gw[g][l][:].bitcast(U32), xw[g][:].bitcast(U32).indirect(lists[l][:]))
+            nc.vector.tensor_copy(gw[g][:, l, :].bitcast(U32), xw[g][:].bitcast(U32).indirect(lists[l][:]))
 
         def gather_scales(l):
-            gs[l] = sb("wb0" if l else "gs0", [P, S], U8)
             nc.vector.tensor_copy(gs[l][:], xs[:].indirect(lists[l][:]))
 
-        def deal(g, h, m0, m1, on_vector):
-            dst = wb[g][:, :, m0:m1, 2 * h:2 * h + 2].rearrange("p t m j -> p m j t")
-            src = raw[g, h][:, :, PACK * m0:PACK * m1].rearrange("p j (m t) -> p m j t", t=PACK)
+        def deal(g, m0, m1, on_vector):
+            dst = wb[g][:, :, m0:m1, :].rearrange("p t m j -> p m j t")
+            src = raw[g][:, :, PACK * m0:PACK * m1].rearrange("p j (m t) -> p m j t", t=PACK)
             if on_vector:
                 nc.vector.tensor_copy(dst, src)
             else:
@@ -94,29 +93,29 @@ def tile_picked_yadain_none_po_kernel(tc, x_words, x_scales, w1, offs, style, ou
                 out=acc[l][t][:],
                 lhsT=wq[g][:, P * t:P * (t + 1)].bitcast(FP8X4),
                 lhsT_scale=ws[g][:, P * t:P * (t + 1)],
-                rhs=gw[g][l][:].bitcast(FP8X4),
+                rhs=gw[g][:, l, :].bitcast(FP8X4),
                 rhs_scale=gs[l][4 * g:P, :],
                 start=(g == 0),
                 stop=(g == PASSES - 1),
             )
 
+        gw[0] = sb("gw0", [P, 2, S], I32)
         gather_words(0, 0)
         gather_words(0, 1)
         gather_scales(0)
-        deal(0, 0, 0, P, False)
-        load_w(1, 0)
-        deal(0, 1, 0, P, False)
-        load_w(1, 1)
-        quant_w(0, 0, PACK)
         gather_scales(1)
+        deal(0, 0, P, False)
+        wq[0] = sb("xs", [P, N], U32)
+        quant_w(0, 0, PACK)
         for l in range(2):
             for t in range(PACK):
                 mm(0, l, t)
+        gw[1] = sb("wb0", [P, 2, S], I32)
         gather_words(1, 0)
         gather_words(1, 1)
-        deal(1, 0, 0, P, False)
-        deal(1, 1, 0, 56, True)
-        deal(1, 1, 56, P, False)
+        deal(1, 0, 72, True)
+        deal(1, 72, P, False)
+        wq[1] = sb("wq1", [P, N], U32)
         for t in range(PACK):
             quant_w(1, t, t + 1)
         for l, t in ((0, 0), (1, 0), (0, 1), (1, 1), (0, 2), (0, 3), (1, 2), (1, 3)):
@@ -147,7 +146,7 @@ def tile_picked_yadain_none_po_kernel(tc, x_words, x_scales, w1, offs, style, ou
 
         def inverse(u):
             nc.vector.reciprocal(ry[u][:], vye[u][:])
-            nc.vector.tensor_scalar(er[u][:], ry[u][:], EPS, None, ALU.mult)
+            nc.scalar.activation(er[u][:], ry[u][:], ACT.Copy, scale=EPS)
 
         def factors(t):
             u, i = divmod(t, 2)
@@ -166,31 +165,32 @@ def tile_picked_yadain_none_po_kernel(tc, x_words, x_scales, w1, offs, style, ou
         stats(1, 0, mvz[0][:])
         stats(1, 1, mvz[1][:])
         stats(0, 2, mvy[:, 0, :])
-        nc.vector.tensor_scalar(vye[0][:], m2y[:], 1.0 / S, EPS, ALU.mult, ALU.add)
+        nc.scalar.activation(vye[0][:], m2y[:], ACT.Copy, scale=1.0 / S, bias=EPS)
         inverse(0)
         for t in range(2):
             factors(t)
             affine(t, 0, S, False)
             store(t)
         stats(0, 3, mvy[:, 1, :])
-        nc.vector.tensor_scalar(vye[1][:], mvy[:, :, 1], EPS, None, ALU.add)
-        nc.vector.tensor_scalar(negmy[:, 2:4], mvy[:, :, 0], -1.0, None, ALU.mult)
-        inverse(1)
+        nc.scalar.activation(vye[1][:], mvy[:, :, 1], ACT.Copy, bias=EPS)
+        nc.scalar.activation(negmy[:, 2:4], mvy[:, :, 0], ACT.Copy, scale=-1.0)
         stats(1, 2, mvz[2][:])
+        inverse(1)
         factors(2)
-        affine(2, 0, S, False)
-        store(2)
         stats(1, 3, mvz[3][:])
         factors(3)
-        affine(3, 0, S, True)
+        affine(2, 0, S, True)
+        store(2)
+        affine(3, 0, S // 2, False)
+        affine(3, S // 2, S, False)
         store(3)
 
-        rb = sb("rb", [P, S, PACK], BF16)
+        rb = [sb("rb%d" % h, [P, S // 2, PACK], BF16) for h in range(2)]
         oq = sb("oq", [P, S], U32)
         osc = sb("osc", [P, S], U8)
 
         def weave(c0, c1, on_vector):
-            dst = rb[:, c0:c1, :].rearrange("p (c i) t -> p c t i", i=4)
+            dst = rb[c0 // 256][:, c0 % 256:(c1 - 1) % 256 + 1, :].rearrange("p (c i) t -> p c t i", i=4)
             src = res[:, :, c0:c1].rearrange("p t (c i) -> p c t i", i=4)
             if on_vector:
                 nc.vector.tensor_copy(dst, src)
@@ -201,7 +201,7 @@ def tile_picked_yadain_none_po_kernel(tc, x_words, x_scales, w1, offs, style, ou
             nc.vector.quantize_mx(
                 out=oq[:, c0:c1].bitcast(FP8X4),
                 scales=osc[:, c0:c1],
-                in_=rb[:, c0:c1, :].rearrange("p c t -> p (c t)"),
+                in_=rb[c0 // 256][:].rearrange("p c t -> p (c t)"),
             )
             words = out_1[0].rearrange("p n t -> p (n t)").bitcast(I32)
             nc.sync.dma_start(words[:, c0:c1], oq[:, c0:c1].bitcast(I32))

@@ -44,36 +44,40 @@ def tile_picked_yadain_none_po_kernel(tc, x_words, x_scales, w1, offs, style, ou
         def load_x(g):
             nc.sync.dma_start(xw[g][:], x_words[g].rearrange("p n t -> p (n t)").bitcast(I32))
 
-        def load_w(g):
+        def load_w(g, m0, m1):
             rows = w1[g * P * PACK:(g + 1) * P * PACK, :].rearrange("(p j) c -> p j c", j=PACK)
-            raw[g] = sb("raw%d" % g, [P, PACK, N], F32)
-            nc.sync.dma_start(raw[g][:], rows)
+            raw[g, m0] = sb("raw%d_%d" % (g, m0), [P, PACK, PACK * (m1 - m0)], F32)
+            nc.sync.dma_start(raw[g, m0][:], rows[:, :, PACK * m0:PACK * m1])
 
         nc.sync.dma_start(lists[0][:], offs)
         nc.sync.dma_start(lists[1][:], style)
-        load_x(0)
+        load_w(0, 0, 64)
         for q in range(QUADS):
-            nc.scalar.dma_start(xs[32 * q:32 * q + 4 * PASSES, :].bitcast(I32), x_scales[:, 4 * q:4 * q + 4, :].bitcast(I32))
+            nc.sync.dma_start(xs[32 * q:32 * q + 4 * PASSES, :].bitcast(I32), x_scales[:, 4 * q:4 * q + 4, :].bitcast(I32))
         nc.scalar.activation(warm2[:], warm[:], ACT.Sqrt)
-        load_w(0)
+        load_x(0)
+        load_w(0, 64, P)
         load_x(1)
-        load_w(1)
+        load_w(1, 0, 64)
+        load_w(1, 64, P)
 
         gw = {}
-        gs = [sb("gs%d" % l, [P, S], U8) for l in range(2)]
+        gs = {}
         wb = [sb("wb%d" % g, [P, PACK, P, PACK], BF16) for g in range(PASSES)]
         wq = {}
         ws = [sb("ws%d" % g, [P, N], U8) for g in range(PASSES)]
 
         def gather_words(g, l):
-            nc.vector.tensor_copy(gw[g][:, l, :].bitcast(U32), xw[g][:].bitcast(U32).indirect(lists[l][:]))
+            gw[g, l] = sb("wb0" if (g, l) == (1, 0) else "gw%d%d" % (g, l), [P, S], I32)
+            nc.vector.tensor_copy(gw[g, l][:].bitcast(U32), xw[g][:].bitcast(U32).indirect(lists[l][:]))
 
         def gather_scales(l):
+            gs[l] = sb("gs%d" % l, [P, S], U8)
             nc.vector.tensor_copy(gs[l][:], xs[:].indirect(lists[l][:]))
 
-        def deal(g, m0, m1, on_vector):
+        def deal(g, base, m0, m1, on_vector):
             dst = wb[g][:, :, m0:m1, :].rearrange("p t m j -> p m j t")
-            src = raw[g][:, :, PACK * m0:PACK * m1].rearrange("p j (m t) -> p m j t", t=PACK)
+            src = raw[g, base][:, :, PACK * (m0 - base):PACK * (m1 - base)].rearrange("p j (m t) -> p m j t", t=PACK)
             if on_vector:
                 nc.vector.tensor_copy(dst, src)
             else:
@@ -93,97 +97,100 @@ def tile_picked_yadain_none_po_kernel(tc, x_words, x_scales, w1, offs, style, ou
                 out=acc[l][t][:],
                 lhsT=wq[g][:, P * t:P * (t + 1)].bitcast(FP8X4),
                 lhsT_scale=ws[g][:, P * t:P * (t + 1)],
-                rhs=gw[g][:, l, :].bitcast(FP8X4),
+                rhs=gw[g, l][:].bitcast(FP8X4),
                 rhs_scale=gs[l][4 * g:P, :],
                 start=(g == 0),
                 stop=(g == PASSES - 1),
             )
 
-        gw[0] = sb("gw0", [P, 2, S], I32)
-        gather_words(0, 0)
-        gather_words(0, 1)
         gather_scales(0)
         gather_scales(1)
-        deal(0, 0, P, False)
-        wq[0] = sb("xs", [P, N], U32)
-        quant_w(0, 0, PACK)
+        gather_words(0, 0)
+        gather_words(0, 1)
+        deal(0, 0, 0, 64, False)
+        deal(0, 64, 64, P, False)
+        wq[0] = sb("wq0", [P, N], U32)
+        quant_w(0, 0, 1)
+        quant_w(0, 1, 2)
+        quant_w(0, 2, PACK)
         for l in range(2):
             for t in range(PACK):
                 mm(0, l, t)
-        gw[1] = sb("wb0", [P, 2, S], I32)
         gather_words(1, 0)
         gather_words(1, 1)
-        deal(1, 0, 72, True)
-        deal(1, 72, P, False)
+        deal(1, 0, 0, 64, False)
+        deal(1, 64, 64, 104, True)
+        deal(1, 64, 104, P, False)
         wq[1] = sb("wq1", [P, N], U32)
-        for t in range(PACK):
+        for t in (0, 2, 1, 3):
             quant_w(1, t, t + 1)
-        for l, t in ((0, 0), (1, 0), (0, 1), (1, 1), (0, 2), (0, 3), (1, 2), (1, 3)):
+        for l, t in ((0, 0), (0, 2), (0, 1), (0, 3), (1, 2), (1, 3), (1, 0), (1, 1)):
             mm(1, l, t)
 
-        junk = [sb("junk%d" % i, [P, S], BF16) for i in range(4)]
-        negmy = sb("negmy", [P, PACK], F32)
+        ysb = [sb("ysb%d" % t, [P, S], F32) for t in range(2)]
+        junk = [sb("junk%d" % t, [P, S], BF16) for t in range(2)]
+        sumy = sb("sumy", [P, 2], F32)
         m2y = sb("m2y", [P, 2], F32)
+        negmy = sb("negmy", [P, PACK], F32)
         st = [[sb("st%d%d" % (l, t), [P, 6], F32) for t in range(PACK)] for l in range(2)]
         mvy = sb("mvy", [P, 2, 2], F32)
         mvz = [sb("mvz%d" % t, [P, 2], F32) for t in range(PACK)]
-        vye = [sb("vye%d" % u, [P, 2], F32) for u in range(2)]
-        ry = [sb("ry%d" % u, [P, 2], F32) for u in range(2)]
-        er = [sb("er%d" % u, [P, 2], F32) for u in range(2)]
+        vye = sb("vye", [P, PACK], F32)
+        ry = sb("ry", [P, PACK], F32)
+        er = sb("er", [P, PACK], F32)
         f = [sb("f%d" % t, [P, 1], F32) for t in range(PACK)]
         b = [sb("b%d" % t, [P, 1], F32) for t in range(PACK)]
         res = sb("res", [P, PACK, S], F32)
         out_rows = out_0.rearrange("(p t) c -> p t c", t=PACK)
 
         for t in range(2):
-            nc.scalar.activation(junk[t][:], acc[0][t][:], ACT.Identity, scale=-1.0 / S, accum_out=negmy[:, t:t + 1])
+            nc.scalar.activation(ysb[t][:], acc[0][t][:], ACT.Identity, accum_out=sumy[:, t:t + 1])
         for t in range(2):
-            nc.scalar.activation(junk[2 + t][:], acc[0][t][:], ACT.Square, bias=negmy[:, t:t + 1], accum_out=m2y[:, t:t + 1])
+            nc.scalar.activation(junk[t][:], acc[0][t][:], ACT.Square, scale=-float(S), bias=sumy[:, t:t + 1], accum_out=m2y[:, t:t + 1])
 
-        def stats(l, t, mv):
+        def stats(l, t):
             nc.vector.bn_stats(st[l][t][:], acc[l][t][:])
-            nc.vector.bn_aggr(mv, st[l][t][:])
 
-        def inverse(u):
-            nc.vector.reciprocal(ry[u][:], vye[u][:])
-            nc.scalar.activation(er[u][:], ry[u][:], ACT.Copy, scale=EPS)
+        def aggr(l, t):
+            nc.vector.bn_aggr(mvz[t][:] if l else mvy[:, t - 2, :], st[l][t][:])
 
-        def factors(t):
-            u, i = divmod(t, 2)
-            nc.scalar.activation(f[t][:], mvz[t][:, 1:2], ACT.Sqrt, scale=ry[u][:, i:i + 1], bias=er[u][:, i:i + 1])
-            nc.scalar.activation(b[t][:], f[t][:], ACT.Identity, scale=negmy[:, t:t + 1], bias=mvz[t][:, 0:1])
+        def factors(ts):
+            for t in ts:
+                nc.scalar.activation(f[t][:], mvz[t][:, 1:2], ACT.Sqrt, scale=ry[:, t:t + 1], bias=er[:, t:t + 1])
+            for t in ts:
+                nc.scalar.activation(b[t][:], f[t][:], ACT.Identity, scale=negmy[:, t:t + 1], bias=mvz[t][:, 0:1])
 
-        def affine(t, c0, c1, on_vector):
-            if on_vector:
-                nc.vector.tensor_scalar(res[:, t, c0:c1], acc[0][t][:, c0:c1], f[t][:], b[t][:], ALU.mult, ALU.add)
+        def affine(t):
+            if t < 2:
+                nc.vector.tensor_scalar(res[:, t, :], ysb[t][:], f[t][:], b[t][:], ALU.mult, ALU.add)
             else:
-                nc.scalar.activation(res[:, t, c0:c1], acc[0][t][:, c0:c1], ACT.Identity, scale=f[t][:], bias=b[t][:])
-
-        def store(t):
+                nc.scalar.activation(res[:, t, :], acc[0][t][:], ACT.Identity, scale=f[t][:], bias=b[t][:])
             nc.sync.dma_start(out_rows[:, t, :], res[:, t, :])
 
-        stats(1, 0, mvz[0][:])
-        stats(1, 1, mvz[1][:])
-        stats(0, 2, mvy[:, 0, :])
-        nc.scalar.activation(vye[0][:], m2y[:], ACT.Copy, scale=1.0 / S, bias=EPS)
-        inverse(0)
-        for t in range(2):
-            factors(t)
-            affine(t, 0, S, False)
-            store(t)
-        stats(0, 3, mvy[:, 1, :])
-        nc.scalar.activation(vye[1][:], mvy[:, :, 1], ACT.Copy, bias=EPS)
+        stats(0, 2)
+        stats(0, 3)
+        aggr(0, 2)
+        stats(1, 2)
+        aggr(0, 3)
+        nc.scalar.activation(vye[:, 2:4], mvy[:, :, 1], ACT.Copy, bias=EPS)
+        nc.scalar.activation(vye[:, 0:2], m2y[:], ACT.Copy, scale=1.0 / S ** 3, bias=EPS)
         nc.scalar.activation(negmy[:, 2:4], mvy[:, :, 0], ACT.Copy, scale=-1.0)
-        stats(1, 2, mvz[2][:])
-        inverse(1)
-        factors(2)
-        stats(1, 3, mvz[3][:])
-        factors(3)
-        affine(2, 0, S, True)
-        store(2)
-        affine(3, 0, S // 2, False)
-        affine(3, S // 2, S, False)
-        store(3)
+        nc.scalar.activation(negmy[:, 0:2], sumy[:], ACT.Copy, scale=-1.0 / S)
+        stats(1, 3)
+        aggr(1, 2)
+        nc.vector.reciprocal(ry[:], vye[:])
+        aggr(1, 3)
+        nc.scalar.activation(er[:], ry[:], ACT.Copy, scale=EPS)
+        stats(1, 0)
+        stats(1, 1)
+        aggr(1, 0)
+        aggr(1, 1)
+        factors((2, 3))
+        affine(2)
+        factors((0, 1))
+        affine(3)
+        affine(0)
+        affine(1)
 
         rb = [sb("rb%d" % h, [P, S // 2, PACK], BF16) for h in range(2)]
         oq = sb("oq", [P, S], U32)

@@ -38,7 +38,12 @@ def tile_picked_yadain_none_po_kernel(tc, x_words, x_scales, w1, offs, style, ou
 
         warm = sb("warm", [P, 1], F32)
         warm2 = sb("warm2", [P, 1], F32)
-        nc.vector.memset(xs[:].bitcast(I32), 0)
+        nc.vector.memset(xs[32:64, :].bitcast(I32), 0)
+        nc.vector.memset(xs[64:P, :].bitcast(I32), 0)
+        planes = [sb("plane%d" % g, [P, 2 * S], U8) for g in range(PASSES)]
+        for g in range(PASSES):
+            nc.gpsimd.memset(planes[g][:].bitcast(I32), 0)
+        picked = sb("picked", [P, 2 * S], U8)
         nc.vector.memset(warm[:], 1.0)
 
         def load_x(g):
@@ -51,18 +56,16 @@ def tile_picked_yadain_none_po_kernel(tc, x_words, x_scales, w1, offs, style, ou
 
         nc.sync.dma_start(lists[0][:], offs)
         nc.sync.dma_start(lists[1][:], style)
-        load_w(0, 0, 64)
-        for q in range(QUADS):
-            nc.sync.dma_start(xs[32 * q:32 * q + 4 * PASSES, :].bitcast(I32), x_scales[:, 4 * q:4 * q + 4, :].bitcast(I32))
+        nc.sync.dma_start(xs[0:32, :].bitcast(I32), x_scales.rearrange("g q n -> (g q) n").bitcast(I32))
         nc.scalar.activation(warm2[:], warm[:], ACT.Sqrt)
         load_x(0)
+        load_w(0, 0, 64)
         load_w(0, 64, P)
         load_x(1)
         load_w(1, 0, 64)
         load_w(1, 64, P)
 
         gw = {}
-        gs = {}
         wb = [sb("wb%d" % g, [P, PACK, P, PACK], BF16) for g in range(PASSES)]
         wq = {}
         ws = [sb("ws%d" % g, [P, N], U8) for g in range(PASSES)]
@@ -72,8 +75,11 @@ def tile_picked_yadain_none_po_kernel(tc, x_words, x_scales, w1, offs, style, ou
             nc.vector.tensor_copy(gw[g, l][:].bitcast(U32), xw[g][:].bitcast(U32).indirect(lists[l][:]))
 
         def gather_scales(l):
-            gs[l] = sb("gs%d" % l, [P, S], U8)
-            nc.vector.tensor_copy(gs[l][:], xs[:].indirect(lists[l][:]))
+            nc.vector.tensor_copy(picked[:, S * l:S * (l + 1)], xs[:].indirect(lists[l][:]))
+
+        def place_scales(g, eng):
+            for q in range(QUADS):
+                eng.dma_start(planes[g][32 * q:32 * q + 4, :].bitcast(I32), picked[16 * g + 4 * q:16 * g + 4 * q + 4, :].bitcast(I32))
 
         def deal(g, base, m0, m1, on_vector):
             dst = wb[g][:, :, m0:m1, :].rearrange("p t m j -> p m j t")
@@ -98,13 +104,15 @@ def tile_picked_yadain_none_po_kernel(tc, x_words, x_scales, w1, offs, style, ou
                 lhsT=wq[g][:, P * t:P * (t + 1)].bitcast(FP8X4),
                 lhsT_scale=ws[g][:, P * t:P * (t + 1)],
                 rhs=gw[g, l][:].bitcast(FP8X4),
-                rhs_scale=gs[l][4 * g:P, :],
+                rhs_scale=planes[g][:, S * l:S * (l + 1)],
                 start=(g == 0),
                 stop=(g == PASSES - 1),
             )
 
         gather_scales(0)
         gather_scales(1)
+        place_scales(0, nc.scalar)
+        place_scales(1, nc.gpsimd)
         gather_words(0, 0)
         gather_words(0, 1)
         deal(0, 0, 0, 64, False)

@@ -20,6 +20,7 @@ P = 128
 PACK = 4
 PASSES = K // (P * PACK)
 QUADS = 4
+ROWS = 16
 
 
 def tile_picked_yadain_none_po_kernel(tc, x_words, x_scales, w1, offs, style, out_0, out_1, out_2):
@@ -35,35 +36,40 @@ def tile_picked_yadain_none_po_kernel(tc, x_words, x_scales, w1, offs, style, ou
         xs = sb("xs", [P, T], U8)
         xw = [sb("xw%d" % g, [P, T], I32) for g in range(PASSES)]
         raw = {}
+        planes = [sb("plane%d" % g, [P, 2 * S], U8) for g in range(PASSES)]
+        picked = sb("picked", [P, 2 * S], U8)
 
-        warm = sb("warm", [P, 1], F32)
-        warm2 = sb("warm2", [P, 1], F32)
         nc.vector.memset(xs[32:64, :].bitcast(I32), 0)
         nc.vector.memset(xs[64:P, :].bitcast(I32), 0)
-        planes = [sb("plane%d" % g, [P, 2 * S], U8) for g in range(PASSES)]
         for g in range(PASSES):
             nc.gpsimd.memset(planes[g][:].bitcast(I32), 0)
-        picked = sb("picked", [P, 2 * S], U8)
-        nc.vector.memset(warm[:], 1.0)
+
+        ystat = sb("ystat", [P, PACK, 8], F32)
+        zstat = sb("zstat", [P, PACK, 8], F32)
+        one = sb("one", [P, 1], F32)
+        nc.gpsimd.memset(one[:], 1.0)
+        nc.gpsimd.memset(zstat[:], 0.0)
+        nc.gpsimd.memset(ystat[:, 0:3, 0:1], 1.0 / S)
+        nc.gpsimd.memset(ystat[:, 0:3, 2:3], float(S))
+        nc.gpsimd.memset(ystat[:, 3, 0:3], 1.0)
+        nc.scalar.activation(ystat[:, 0:3, 1], one[:].to_broadcast([P, 3]), ACT.Abs_reciprocal_sqrt, scale=1.0 / (EPS * S * S) ** 2)
+        nc.scalar.activation(ystat[:, 3, 1:2], one[:], ACT.Copy, scale=EPS)
 
         def load_x(g):
             nc.sync.dma_start(xw[g][:], x_words[g].rearrange("p n t -> p (n t)").bitcast(I32))
 
         def load_w(g, m0, m1):
             rows = w1[g * P * PACK:(g + 1) * P * PACK, :].rearrange("(p j) c -> p j c", j=PACK)
-            raw[g, m0] = sb("raw%d_%d" % (g, m0), [P, PACK, PACK * (m1 - m0)], F32)
+            raw[g, m0] = sb("raw%d" % m0, [P, PACK, PACK * (m1 - m0)], F32)
             nc.sync.dma_start(raw[g, m0][:], rows[:, :, PACK * m0:PACK * m1])
 
         nc.sync.dma_start(lists[0][:], offs)
         nc.sync.dma_start(lists[1][:], style)
-        nc.sync.dma_start(xs[0:32, :].bitcast(I32), x_scales.rearrange("g q n -> (g q) n").bitcast(I32))
-        nc.scalar.activation(warm2[:], warm[:], ACT.Sqrt)
+        nc.sync.dma_start(xs[0:PASSES * ROWS, :].bitcast(I32), x_scales.rearrange("g q n -> (g q) n").bitcast(I32))
         load_x(0)
         load_w(0, 0, 64)
         load_w(0, 64, P)
         load_x(1)
-        load_w(1, 0, 64)
-        load_w(1, 64, P)
 
         gw = {}
         wb = [sb("wb%d" % g, [P, PACK, P, PACK], BF16) for g in range(PASSES)]
@@ -79,7 +85,8 @@ def tile_picked_yadain_none_po_kernel(tc, x_words, x_scales, w1, offs, style, ou
 
         def place_scales(g, eng):
             for q in range(QUADS):
-                eng.dma_start(planes[g][32 * q:32 * q + 4, :].bitcast(I32), picked[16 * g + 4 * q:16 * g + 4 * q + 4, :].bitcast(I32))
+                src = picked[ROWS * g + 4 * q:ROWS * g + 4 * q + 4, :]
+                eng.dma_start(planes[g][32 * q:32 * q + 4, :].bitcast(I32), src.bitcast(I32))
 
         def deal(g, base, m0, m1, on_vector):
             dst = wb[g][:, :, m0:m1, :].rearrange("p t m j -> p m j t")
@@ -117,6 +124,8 @@ def tile_picked_yadain_none_po_kernel(tc, x_words, x_scales, w1, offs, style, ou
         gather_words(0, 1)
         deal(0, 0, 0, 64, False)
         deal(0, 64, 64, P, False)
+        load_w(1, 0, 64)
+        load_w(1, 64, P)
         wq[0] = sb("wq0", [P, N], U32)
         quant_w(0, 0, 1)
         quant_w(0, 1, 2)
@@ -130,75 +139,85 @@ def tile_picked_yadain_none_po_kernel(tc, x_words, x_scales, w1, offs, style, ou
         deal(1, 64, 64, 104, True)
         deal(1, 64, 104, P, False)
         wq[1] = sb("wq1", [P, N], U32)
-        for t in (0, 2, 1, 3):
+        for t in (0, 3, 1, 2):
             quant_w(1, t, t + 1)
-        for l, t in ((0, 0), (0, 2), (0, 1), (0, 3), (1, 2), (1, 3), (1, 0), (1, 1)):
+        for l, t in ((0, 0), (0, 3), (0, 1), (1, 3), (0, 2), (1, 0), (1, 1), (1, 2)):
             mm(1, l, t)
 
-        ysb = [sb("ysb%d" % t, [P, S], F32) for t in range(2)]
-        junk = [sb("junk%d" % t, [P, S], BF16) for t in range(2)]
-        sumy = sb("sumy", [P, 2], F32)
-        m2y = sb("m2y", [P, 2], F32)
-        negmy = sb("negmy", [P, PACK], F32)
+        ysb = [sb("ysb%d" % t, [P, S], F32) for t in range(3)]
+        junk = sb("junk", [P, 3, S], BF16)
+        m2y = sb("m2y", [P, 3], F32)
         st = [[sb("st%d%d" % (l, t), [P, 6], F32) for t in range(PACK)] for l in range(2)]
-        mvy = sb("mvy", [P, 2, 2], F32)
-        mvz = [sb("mvz%d" % t, [P, 2], F32) for t in range(PACK)]
-        vye = sb("vye", [P, PACK], F32)
-        ry = sb("ry", [P, PACK], F32)
-        er = sb("er", [P, PACK], F32)
-        f = [sb("f%d" % t, [P, 1], F32) for t in range(PACK)]
-        b = [sb("b%d" % t, [P, 1], F32) for t in range(PACK)]
+        prod = [sb("prod%d" % t, [P, 4], F32) for t in range(PACK)]
+        inv = [sb("inv%d" % t, [P, 1], F32) for t in range(PACK)]
+        gain = [sb("gain%d" % t, [P, 2], F32) for t in range(PACK)]
+        shift = sb("shift", [P, 1], F32)
         res = sb("res", [P, PACK, S], F32)
         out_rows = out_0.rearrange("(p t) c -> p t c", t=PACK)
 
-        for t in range(2):
-            nc.scalar.activation(ysb[t][:], acc[0][t][:], ACT.Identity, accum_out=sumy[:, t:t + 1])
-        for t in range(2):
-            nc.scalar.activation(junk[t][:], acc[0][t][:], ACT.Square, scale=-float(S), bias=sumy[:, t:t + 1], accum_out=m2y[:, t:t + 1])
+        def first_read(t):
+            nc.scalar.activation(ysb[t][:], acc[0][t][:], ACT.Identity, accum_out=ystat[:, t, 3:4])
+
+        def second_read(t):
+            nc.scalar.activation(junk[:, t, :], acc[0][t][:], ACT.Square, scale=-float(S), bias=ystat[:, t, 3:4], accum_out=m2y[:, t:t + 1])
 
         def stats(l, t):
             nc.vector.bn_stats(st[l][t][:], acc[l][t][:])
 
         def aggr(l, t):
-            nc.vector.bn_aggr(mvz[t][:] if l else mvy[:, t - 2, :], st[l][t][:])
+            nc.vector.bn_aggr(zstat[:, t, 1:3] if l else ystat[:, t, 3:5], st[l][t][:])
 
-        def factors(ts):
-            for t in ts:
-                nc.scalar.activation(f[t][:], mvz[t][:, 1:2], ACT.Sqrt, scale=ry[:, t:t + 1], bias=er[:, t:t + 1])
-            for t in ts:
-                nc.scalar.activation(b[t][:], f[t][:], ACT.Identity, scale=negmy[:, t:t + 1], bias=mvz[t][:, 0:1])
+        def products(t):
+            nc.vector.scalar_tensor_tensor(prod[t][:], zstat[:, t, 2:3].to_broadcast([P, 4]), EPS, ystat[:, t, 0:4], ALU.add, ALU.mult)
 
-        def affine(t):
-            if t < 2:
-                nc.vector.tensor_scalar(res[:, t, :], ysb[t][:], f[t][:], b[t][:], ALU.mult, ALU.add)
-            else:
-                nc.scalar.activation(res[:, t, :], acc[0][t][:], ACT.Identity, scale=f[t][:], bias=b[t][:])
+        def root(t):
+            spread = m2y[:, t:t + 1] if t < 3 else ystat[:, t, 4:5]
+            nc.scalar.activation(inv[t][:], spread, ACT.Abs_reciprocal_sqrt, scale=prod[t][:, 0:1], bias=prod[t][:, 1:2])
+
+        def gains(t):
+            nc.vector.scalar_tensor_tensor(gain[t][:], prod[t][:, 2:4], inv[t][:], zstat[:, t, 0:2], ALU.mult, ALU.subtract)
+
+        def affine(t, eng):
+            eng.tensor_scalar(res[:, t, :], ysb[t][:], gain[t][:, 0:1], gain[t][:, 1:2], ALU.mult, ALU.subtract)
             nc.sync.dma_start(out_rows[:, t, :], res[:, t, :])
 
-        stats(0, 2)
+        def affine_psum(t):
+            nc.vector.tensor_scalar(shift[:], gain[t][:, 1:2], -1.0, None, ALU.mult)
+            nc.scalar.activation(res[:, t, :], acc[0][t][:], ACT.Identity, scale=gain[t][:, 0:1], bias=shift[:])
+            nc.sync.dma_start(out_rows[:, t, :], res[:, t, :])
+
+        first_read(0)
+        first_read(1)
+        second_read(0)
+        first_read(2)
         stats(0, 3)
-        aggr(0, 2)
-        stats(1, 2)
-        aggr(0, 3)
-        nc.scalar.activation(vye[:, 2:4], mvy[:, :, 1], ACT.Copy, bias=EPS)
-        nc.scalar.activation(vye[:, 0:2], m2y[:], ACT.Copy, scale=1.0 / S ** 3, bias=EPS)
-        nc.scalar.activation(negmy[:, 2:4], mvy[:, :, 0], ACT.Copy, scale=-1.0)
-        nc.scalar.activation(negmy[:, 0:2], sumy[:], ACT.Copy, scale=-1.0 / S)
         stats(1, 3)
-        aggr(1, 2)
-        nc.vector.reciprocal(ry[:], vye[:])
-        aggr(1, 3)
-        nc.scalar.activation(er[:], ry[:], ACT.Copy, scale=EPS)
+        aggr(0, 3)
         stats(1, 0)
-        stats(1, 1)
+        aggr(1, 3)
         aggr(1, 0)
+        products(3)
+        products(0)
+        root(3)
+        root(0)
+        stats(1, 1)
+        gains(3)
+        gains(0)
+        affine_psum(3)
+        second_read(1)
+        second_read(2)
         aggr(1, 1)
-        factors((2, 3))
-        affine(2)
-        factors((0, 1))
-        affine(3)
-        affine(0)
-        affine(1)
+        affine(0, nc.vector)
+        stats(1, 2)
+        products(1)
+        aggr(1, 2)
+        root(1)
+        products(2)
+        root(2)
+        gains(1)
+        affine(1, nc.vector)
+        gains(2)
+        affine(2, nc.vector)
 
         rb = [sb("rb%d" % h, [P, S // 2, PACK], BF16) for h in range(2)]
         oq = sb("oq", [P, S], U32)
@@ -222,8 +241,8 @@ def tile_picked_yadain_none_po_kernel(tc, x_words, x_scales, w1, offs, style, ou
             nc.sync.dma_start(words[:, c0:c1], oq[:, c0:c1].bitcast(I32))
 
         weave(0, 256, True)
-        weave(384, S, False)
-        weave(256, 384, True)
+        weave(352, S, False)
+        weave(256, 352, True)
         quant_out(0, 256)
         quant_out(256, S)
         for q in range(QUADS):

@@ -27,6 +27,7 @@ def tile_picked_yadain_none_po_kernel(tc, x_words, x_scales, w1, offs, style, ou
     nc = tc.nc
     with ExitStack() as ctx:
         keep = ctx.enter_context(tc.tile_pool(name="keep", bufs=1))
+        reuse = ctx.enter_context(tc.tile_pool(name="reuse", bufs=1))
         psum = ctx.enter_context(tc.psum_pool(name="psum", bufs=1))
 
         def sb(name, shape, dtype):
@@ -36,13 +37,12 @@ def tile_picked_yadain_none_po_kernel(tc, x_words, x_scales, w1, offs, style, ou
         xs = sb("xs", [P, T], U8)
         xw = [sb("xw%d" % g, [P, T], I32) for g in range(PASSES)]
         raw = {}
-        planes = [sb("plane%d" % g, [P, 2 * S], U8) for g in range(PASSES)]
+        planes = [sb("plane0", [P, 2 * S], U8)]
         picked = sb("picked", [P, 2 * S], U8)
 
         nc.vector.memset(xs[32:64, :].bitcast(I32), 0)
         nc.vector.memset(xs[64:P, :].bitcast(I32), 0)
-        for g in range(PASSES):
-            nc.gpsimd.memset(planes[g][:].bitcast(I32), 0)
+        nc.gpsimd.memset(planes[0][:].bitcast(I32), 0)
 
         ystat = sb("ystat", [P, PACK, 8], F32)
         zstat = sb("zstat", [P, PACK, 8], F32)
@@ -72,12 +72,15 @@ def tile_picked_yadain_none_po_kernel(tc, x_words, x_scales, w1, offs, style, ou
         load_x(1)
 
         gw = {}
-        wb = [sb("wb%d" % g, [P, PACK, P, PACK], BF16) for g in range(PASSES)]
+        wb = [reuse.tile([P, PACK, P, PACK], BF16, name="wb0", align_bytes=64, offset=0), sb("wb1", [P, PACK, P, PACK], BF16)]
         wq = {}
         ws = [sb("ws%d" % g, [P, N], U8) for g in range(PASSES)]
 
         def gather_words(g, l):
-            gw[g, l] = sb("wb0" if (g, l) == (1, 0) else "gw%d%d" % (g, l), [P, S], I32)
+            if (g, l) == (1, 0):
+                gw[g, l] = reuse.tile([P, S], I32, name="gw10", align_bytes=64, offset=2 * S)
+            else:
+                gw[g, l] = sb("gw%d%d" % (g, l), [P, S], I32)
             nc.vector.tensor_copy(gw[g, l][:].bitcast(U32), xw[g][:].bitcast(U32).indirect(lists[l][:]))
 
         def gather_scales(l):
@@ -119,7 +122,6 @@ def tile_picked_yadain_none_po_kernel(tc, x_words, x_scales, w1, offs, style, ou
         gather_scales(0)
         gather_scales(1)
         place_scales(0, nc.scalar)
-        place_scales(1, nc.gpsimd)
         gather_words(0, 0)
         gather_words(0, 1)
         deal(0, 0, 0, 64, False)
@@ -133,6 +135,9 @@ def tile_picked_yadain_none_po_kernel(tc, x_words, x_scales, w1, offs, style, ou
         for l in range(2):
             for t in range(PACK):
                 mm(0, l, t)
+        planes.append(reuse.tile([P, 2 * S], U8, name="plane1", align_bytes=64, offset=0))
+        nc.vector.memset(planes[1][:].bitcast(I32), 0)
+        place_scales(1, nc.sync)
         gather_words(1, 0)
         gather_words(1, 1)
         deal(1, 0, 0, 64, False)

@@ -21,12 +21,14 @@ PACK = 4
 PASSES = K // (P * PACK)
 QUADS = 4
 ROWS = 16
+M_BYTES = PACK * PACK * 4
 
 
 def tile_picked_yadain_none_po_kernel(tc, x_words, x_scales, w1, offs, style, out_0, out_1, out_2):
     nc = tc.nc
     with ExitStack() as ctx:
         keep = ctx.enter_context(tc.tile_pool(name="keep", bufs=1))
+        stage = ctx.enter_context(tc.tile_pool(name="stage", bufs=1))
         reuse = ctx.enter_context(tc.tile_pool(name="reuse", bufs=1))
         psum = ctx.enter_context(tc.psum_pool(name="psum", bufs=1))
 
@@ -49,39 +51,36 @@ def tile_picked_yadain_none_po_kernel(tc, x_words, x_scales, w1, offs, style, ou
         one = sb("one", [P, 1], F32)
         nc.gpsimd.memset(one[:], 1.0)
         nc.gpsimd.memset(zstat[:], 0.0)
-        nc.gpsimd.memset(ystat[:, 0:3, 0:1], 1.0 / S)
-        nc.gpsimd.memset(ystat[:, 0:3, 2:3], float(S))
-        nc.gpsimd.memset(ystat[:, 3, 0:3], 1.0)
-        nc.scalar.activation(ystat[:, 0:3, 1], one[:].to_broadcast([P, 3]), ACT.Abs_reciprocal_sqrt, scale=1.0 / (EPS * S * S) ** 2)
-        nc.scalar.activation(ystat[:, 3, 1:2], one[:], ACT.Copy, scale=EPS)
+        nc.gpsimd.memset(ystat[:, 1:4, 0:1], 1.0 / S)
+        nc.gpsimd.memset(ystat[:, 1:4, 2:3], -float(S))
+        nc.gpsimd.memset(ystat[:, 0, 0:3], 1.0)
+        nc.scalar.activation(ystat[:, 1:4, 1], one[:].to_broadcast([P, 3]), ACT.Abs_reciprocal_sqrt, scale=1.0 / (EPS * S * S) ** 2)
+        nc.scalar.activation(ystat[:, 0, 1:2], one[:], ACT.Copy, scale=EPS)
 
         def load_x(g):
             nc.sync.dma_start(xw[g][:], x_words[g].rearrange("p n t -> p (n t)").bitcast(I32))
 
-        def load_w(g, m0, m1):
+        def load_w(g, m0, m1, place):
             rows = w1[g * P * PACK:(g + 1) * P * PACK, :].rearrange("(p j) c -> p j c", j=PACK)
-            raw[g, m0] = sb("raw%d" % m0, [P, PACK, PACK * (m1 - m0)], F32)
+            raw[g, m0] = stage.tile([P, PACK, PACK * (m1 - m0)], F32, name="raw%d_%d" % (g, m0), align_bytes=64, offset=place * M_BYTES)
             nc.sync.dma_start(raw[g, m0][:], rows[:, :, PACK * m0:PACK * m1])
 
         nc.sync.dma_start(lists[0][:], offs)
         nc.sync.dma_start(lists[1][:], style)
         nc.sync.dma_start(xs[0:PASSES * ROWS, :].bitcast(I32), x_scales.rearrange("g q n -> (g q) n").bitcast(I32))
         load_x(0)
-        load_w(0, 0, 64)
-        load_w(0, 64, P)
+        load_w(0, 0, 64, 96 - 64)
+        load_w(0, 64, P, 96)
         load_x(1)
 
         gw = {}
         wb = [reuse.tile([P, PACK, P, PACK], BF16, name="wb0", align_bytes=64, offset=0), sb("wb1", [P, PACK, P, PACK], BF16)]
-        wq = {}
+        wq = [sb("wq%d" % g, [P, N], U32) for g in range(PASSES)]
         ws = [sb("ws%d" % g, [P, N], U8) for g in range(PASSES)]
 
-        def gather_words(g, l):
-            if (g, l) == (1, 0):
-                gw[g, l] = reuse.tile([P, S], I32, name="gw10", align_bytes=64, offset=2 * S)
-            else:
-                gw[g, l] = sb("gw%d%d" % (g, l), [P, S], I32)
-            nc.vector.tensor_copy(gw[g, l][:].bitcast(U32), xw[g][:].bitcast(U32).indirect(lists[l][:]))
+        def gather_words(g, l, c0, c1, tile):
+            gw[g, l, c0] = tile
+            nc.vector.tensor_copy(tile[:].bitcast(U32), xw[g][:].bitcast(U32).indirect(lists[l][:, c0 // 16:c1 // 16]))
 
         def gather_scales(l):
             nc.vector.tensor_copy(picked[:, S * l:S * (l + 1)], xs[:].indirect(lists[l][:]))
@@ -108,52 +107,57 @@ def tile_picked_yadain_none_po_kernel(tc, x_words, x_scales, w1, offs, style, ou
 
         acc = [[psum.tile([P, S], F32, name="acc%d%d" % (l, t)) for t in range(PACK)] for l in range(2)]
 
-        def mm(g, l, t):
+        def mm(g, l, t, c0, c1):
             nc.tensor.matmul_mx(
-                out=acc[l][t][:],
+                out=acc[l][t][:, c0:c1],
                 lhsT=wq[g][:, P * t:P * (t + 1)].bitcast(FP8X4),
                 lhsT_scale=ws[g][:, P * t:P * (t + 1)],
-                rhs=gw[g, l][:].bitcast(FP8X4),
-                rhs_scale=planes[g][:, S * l:S * (l + 1)],
+                rhs=gw[g, l, c0][:].bitcast(FP8X4),
+                rhs_scale=planes[g][:, S * l + c0:S * l + c1],
                 start=(g == 0),
-                stop=(g == PASSES - 1),
+                stop=(g == PASSES - 1 and c1 == S),
             )
 
         gather_scales(0)
         gather_scales(1)
         place_scales(0, nc.scalar)
-        gather_words(0, 0)
-        gather_words(0, 1)
+        gather_words(0, 0, 0, S, sb("gw00", [P, S], I32))
+        gather_words(0, 1, 0, S, sb("gw01", [P, S], I32))
         deal(0, 0, 0, 64, False)
         deal(0, 64, 64, P, False)
-        load_w(1, 0, 64)
-        load_w(1, 64, P)
-        wq[0] = sb("wq0", [P, N], U32)
+        load_w(1, 0, 48, 0)
+        load_w(1, 48, 96, 48)
+        load_w(1, 96, P, 96)
         quant_w(0, 0, 1)
         quant_w(0, 1, 2)
         quant_w(0, 2, PACK)
         for l in range(2):
             for t in range(PACK):
-                mm(0, l, t)
+                mm(0, l, t, 0, S)
         planes.append(reuse.tile([P, 2 * S], U8, name="plane1", align_bytes=64, offset=0))
         nc.vector.memset(planes[1][:].bitcast(I32), 0)
         place_scales(1, nc.sync)
-        gather_words(1, 0)
-        gather_words(1, 1)
-        deal(1, 0, 0, 64, False)
-        deal(1, 64, 64, 104, True)
-        deal(1, 64, 104, P, False)
-        wq[1] = sb("wq1", [P, N], U32)
-        for t in (0, 3, 1, 2):
+        gather_words(1, 0, 0, S, reuse.tile([P, S], I32, name="gw10", align_bytes=64, offset=2 * S))
+        gather_words(1, 1, 0, 256, sb("gw11a", [P, 256], I32))
+        deal(1, 0, 0, 48, False)
+        deal(1, 48, 48, 72, True)
+        deal(1, 48, 72, 96, False)
+        deal(1, 96, 96, 118, True)
+        deal(1, 96, 118, P, False)
+        for t in (1, 0, 2, 3):
             quant_w(1, t, t + 1)
-        for l, t in ((0, 0), (0, 3), (0, 1), (1, 3), (0, 2), (1, 0), (1, 1), (1, 2)):
-            mm(1, l, t)
+        gather_words(1, 1, 256, S, stage.tile([P, S - 256], I32, name="gw11b", align_bytes=64, offset=96 * M_BYTES))
+        for t in (1, 0, 2, 3):
+            mm(1, 0, t, 0, S)
+        for t in range(PACK):
+            mm(1, 1, t, 0, 256)
+            mm(1, 1, t, 256, S)
 
-        ysb = [sb("ysb%d" % t, [P, S], F32) for t in range(3)]
-        junk = sb("junk", [P, 3, S], BF16)
-        m2y = sb("m2y", [P, 3], F32)
+        ysb = {t: sb("ysb%d" % t, [P, S], F32) for t in range(1, PACK)}
+        junk = sb("junk", [P, PACK, S], BF16)
+        m2y = sb("m2y", [P, PACK], F32)
         st = [[sb("st%d%d" % (l, t), [P, 6], F32) for t in range(PACK)] for l in range(2)]
-        prod = [sb("prod%d" % t, [P, 4], F32) for t in range(PACK)]
+        prod = sb("prod", [P, PACK, 4], F32)
         inv = [sb("inv%d" % t, [P, 1], F32) for t in range(PACK)]
         gain = [sb("gain%d" % t, [P, 2], F32) for t in range(PACK)]
         shift = sb("shift", [P, 1], F32)
@@ -161,10 +165,10 @@ def tile_picked_yadain_none_po_kernel(tc, x_words, x_scales, w1, offs, style, ou
         out_rows = out_0.rearrange("(p t) c -> p t c", t=PACK)
 
         def first_read(t):
-            nc.scalar.activation(ysb[t][:], acc[0][t][:], ACT.Identity, accum_out=ystat[:, t, 3:4])
+            nc.scalar.activation(ysb[t][:], acc[0][t][:], ACT.Copy, scale=-1.0, accum_out=ystat[:, t, 3:4])
 
         def second_read(t):
-            nc.scalar.activation(junk[:, t, :], acc[0][t][:], ACT.Square, scale=-float(S), bias=ystat[:, t, 3:4], accum_out=m2y[:, t:t + 1])
+            nc.scalar.activation(junk[:, t, :], acc[0][t][:], ACT.Square, scale=float(S), bias=ystat[:, t, 3:4], accum_out=m2y[:, t:t + 1])
 
         def stats(l, t):
             nc.vector.bn_stats(st[l][t][:], acc[l][t][:])
@@ -172,57 +176,63 @@ def tile_picked_yadain_none_po_kernel(tc, x_words, x_scales, w1, offs, style, ou
         def aggr(l, t):
             nc.vector.bn_aggr(zstat[:, t, 1:3] if l else ystat[:, t, 3:5], st[l][t][:])
 
-        def products(t):
-            nc.vector.scalar_tensor_tensor(prod[t][:], zstat[:, t, 2:3].to_broadcast([P, 4]), EPS, ystat[:, t, 0:4], ALU.add, ALU.mult)
+        def products(t0, t1):
+            spread = zstat[:, t0:t1, 2:3].to_broadcast([P, t1 - t0, 4])
+            nc.vector.scalar_tensor_tensor(prod[:, t0:t1, :], spread, EPS, ystat[:, t0:t1, 0:4], ALU.add, ALU.mult)
 
         def root(t):
-            spread = m2y[:, t:t + 1] if t < 3 else ystat[:, t, 4:5]
-            nc.scalar.activation(inv[t][:], spread, ACT.Abs_reciprocal_sqrt, scale=prod[t][:, 0:1], bias=prod[t][:, 1:2])
+            spread = m2y[:, t:t + 1] if t else ystat[:, t, 4:5]
+            nc.scalar.activation(inv[t][:], spread, ACT.Abs_reciprocal_sqrt, scale=prod[:, t, 0:1], bias=prod[:, t, 1:2])
 
         def gains(t):
-            nc.vector.scalar_tensor_tensor(gain[t][:], prod[t][:, 2:4], inv[t][:], zstat[:, t, 0:2], ALU.mult, ALU.subtract)
+            nc.vector.scalar_tensor_tensor(gain[t][:], prod[:, t, 2:4], inv[t][:], zstat[:, t, 0:2], ALU.mult, ALU.add if t else ALU.subtract)
+
+        def store(t):
+            nc.sync.dma_start(out_rows[:, t, :], res[:, t, :])
 
         def affine(t, eng):
-            eng.tensor_scalar(res[:, t, :], ysb[t][:], gain[t][:, 0:1], gain[t][:, 1:2], ALU.mult, ALU.subtract)
-            nc.sync.dma_start(out_rows[:, t, :], res[:, t, :])
+            if eng is nc.scalar:
+                eng.activation(res[:, t, :], ysb[t][:], ACT.Identity, scale=gain[t][:, 0:1], bias=gain[t][:, 1:2])
+            else:
+                eng.tensor_scalar(res[:, t, :], ysb[t][:], gain[t][:, 0:1], gain[t][:, 1:2], ALU.mult, ALU.add)
+            store(t)
 
         def affine_psum(t):
-            nc.vector.tensor_scalar(shift[:], gain[t][:, 1:2], -1.0, None, ALU.mult)
+            nc.scalar.activation(shift[:], gain[t][:, 1:2], ACT.Copy, scale=-1.0)
             nc.scalar.activation(res[:, t, :], acc[0][t][:], ACT.Identity, scale=gain[t][:, 0:1], bias=shift[:])
-            nc.sync.dma_start(out_rows[:, t, :], res[:, t, :])
+            store(t)
 
-        first_read(0)
         first_read(1)
-        second_read(0)
         first_read(2)
-        stats(0, 3)
-        stats(1, 3)
-        aggr(0, 3)
-        stats(1, 0)
-        aggr(1, 3)
-        aggr(1, 0)
-        products(3)
-        products(0)
-        root(3)
-        root(0)
-        stats(1, 1)
-        gains(3)
-        gains(0)
-        affine_psum(3)
         second_read(1)
+        first_read(3)
         second_read(2)
-        aggr(1, 1)
-        affine(0, nc.vector)
+        second_read(3)
+        stats(0, 0)
+        stats(1, 0)
+        aggr(0, 0)
+        stats(1, 1)
+        aggr(1, 0)
         stats(1, 2)
-        products(1)
-        aggr(1, 2)
+        aggr(1, 1)
+        products(0, 2)
         root(1)
-        products(2)
-        root(2)
+        root(0)
+        stats(1, 3)
+        aggr(1, 2)
         gains(1)
-        affine(1, nc.vector)
+        products(2, 3)
+        aggr(1, 3)
+        root(2)
+        gains(0)
+        products(3, 4)
+        root(3)
         gains(2)
+        affine(1, nc.vector)
+        gains(3)
+        affine_psum(0)
         affine(2, nc.vector)
+        affine(3, nc.vector)
 
         rb = [sb("rb%d" % h, [P, S // 2, PACK], BF16) for h in range(2)]
         oq = sb("oq", [P, S], U32)

@@ -187,20 +187,19 @@ def tile_picked_yadain_none_po_kernel(tc, x_words, x_scales, w1, offs, style, ou
         def gains(t):
             nc.vector.scalar_tensor_tensor(gain[t][:], prod[:, t, 2:4], inv[t][:], zstat[:, t, 0:2], ALU.mult, ALU.add if t else ALU.subtract)
 
-        def store(t):
-            nc.sync.dma_start(out_rows[:, t, :], res[:, t, :])
+        def store(t0, t1):
+            nc.sync.dma_start(out_rows[:, t0:t1, :], res[:, t0:t1, :])
 
         def affine(t, eng):
             if eng is nc.scalar:
                 eng.activation(res[:, t, :], ysb[t][:], ACT.Identity, scale=gain[t][:, 0:1], bias=gain[t][:, 1:2])
             else:
                 eng.tensor_scalar(res[:, t, :], ysb[t][:], gain[t][:, 0:1], gain[t][:, 1:2], ALU.mult, ALU.add)
-            store(t)
 
         def affine_psum(t):
             nc.scalar.activation(shift[:], gain[t][:, 1:2], ACT.Copy, scale=-1.0)
             nc.scalar.activation(res[:, t, :], acc[0][t][:], ACT.Identity, scale=gain[t][:, 0:1], bias=shift[:])
-            store(t)
+            store(t, t + 1)
 
         first_read(1)
         first_read(2)
@@ -229,10 +228,12 @@ def tile_picked_yadain_none_po_kernel(tc, x_words, x_scales, w1, offs, style, ou
         root(3)
         gains(2)
         affine(1, nc.vector)
+        store(1, 2)
         gains(3)
         affine_psum(0)
         affine(2, nc.vector)
         affine(3, nc.vector)
+        store(2, PACK)
 
         rb = [sb("rb%d" % h, [P, S // 2, PACK], BF16) for h in range(2)]
         oq = sb("oq", [P, S], U32)
@@ -252,14 +253,13 @@ def tile_picked_yadain_none_po_kernel(tc, x_words, x_scales, w1, offs, style, ou
                 scales=osc[:, c0:c1],
                 in_=rb[c0 // 256][:].rearrange("p c t -> p (c t)"),
             )
-            words = out_1[0].rearrange("p n t -> p (n t)").bitcast(I32)
-            nc.sync.dma_start(words[:, c0:c1], oq[:, c0:c1].bitcast(I32))
 
         weave(0, 256, True)
         weave(352, S, False)
         weave(256, 352, True)
         quant_out(0, 256)
         quant_out(256, S)
+        nc.sync.dma_start(out_1[0].rearrange("p n t -> p (n t)").bitcast(I32), oq[:].bitcast(I32))
         for q in range(QUADS):
             eng = nc.scalar if q % 2 else nc.sync
             eng.dma_start(out_2[0, 4 * q:4 * q + 4, :].bitcast(I32), osc[32 * q:32 * q + 4, :].bitcast(I32))

@@ -29,7 +29,6 @@ def tile_picked_yadain_none_po_kernel(tc, x_words, x_scales, w1, offs, style, ou
     with ExitStack() as ctx:
         keep = ctx.enter_context(tc.tile_pool(name="keep", bufs=1))
         stage = ctx.enter_context(tc.tile_pool(name="stage", bufs=1))
-        reuse = ctx.enter_context(tc.tile_pool(name="reuse", bufs=1))
         psum = ctx.enter_context(tc.psum_pool(name="psum", bufs=1))
 
         def sb(name, shape, dtype):
@@ -74,7 +73,7 @@ def tile_picked_yadain_none_po_kernel(tc, x_words, x_scales, w1, offs, style, ou
         load_x(1)
 
         gw = {}
-        wb = [reuse.tile([P, PACK, P, PACK], BF16, name="wb0", align_bytes=64, offset=0), sb("wb1", [P, PACK, P, PACK], BF16)]
+        wb = [sb("wb%d" % g, [P, PACK, P, PACK], BF16) for g in range(PASSES)]
         wq = [sb("wq%d" % g, [P, N], U32) for g in range(PASSES)]
         ws = [sb("ws%d" % g, [P, N], U8) for g in range(PASSES)]
 
@@ -124,34 +123,30 @@ def tile_picked_yadain_none_po_kernel(tc, x_words, x_scales, w1, offs, style, ou
         gather_words(0, 0, 0, S, sb("gw00", [P, S], I32))
         gather_words(0, 1, 0, S, sb("gw01", [P, S], I32))
         deal(0, 0, 0, 64, False)
-        deal(0, 64, 64, P, False)
+        deal(0, 64, 64, 100, False)
+        deal(0, 64, 100, P, True)
         load_w(1, 0, 48, 0)
         load_w(1, 48, 96, 48)
         load_w(1, 96, P, 96)
         quant_w(0, 0, 1)
         quant_w(0, 1, 2)
         quant_w(0, 2, PACK)
+        planes.append(stage.tile([P, 2 * S], U8, name="plane1", align_bytes=64, offset=P * M_BYTES))
+        nc.vector.memset(planes[1][:].bitcast(I32), 0)
+        place_scales(1, nc.sync)
         for l in range(2):
             for t in range(PACK):
                 mm(0, l, t, 0, S)
-        planes.append(reuse.tile([P, 2 * S], U8, name="plane1", align_bytes=64, offset=0))
-        nc.vector.memset(planes[1][:].bitcast(I32), 0)
-        place_scales(1, nc.sync)
-        gather_words(1, 0, 0, S, reuse.tile([P, S], I32, name="gw10", align_bytes=64, offset=2 * S))
-        gather_words(1, 1, 0, 256, sb("gw11a", [P, 256], I32))
+        gather_words(1, 0, 0, S, sb("gw10", [P, S], I32))
+        gather_words(1, 1, 0, 512, sb("gw11a", [P, 512], I32))
         deal(1, 0, 0, 48, False)
-        deal(1, 48, 48, 72, True)
-        deal(1, 48, 72, 96, False)
-        deal(1, 96, 96, 118, True)
-        deal(1, 96, 118, P, False)
+        deal(1, 48, 48, 96, False)
+        deal(1, 96, 96, 122, True)
+        deal(1, 96, 122, P, False)
         for t in (1, 0, 2, 3):
             quant_w(1, t, t + 1)
-        gather_words(1, 1, 256, S, stage.tile([P, S - 256], I32, name="gw11b", align_bytes=64, offset=96 * M_BYTES))
-        for t in (1, 0, 2, 3):
-            mm(1, 0, t, 0, S)
-        for t in range(PACK):
-            mm(1, 1, t, 0, 256)
-            mm(1, 1, t, 256, S)
+        for l, t in ((0, 1), (0, 0), (0, 2), (1, 0), (0, 3), (1, 1), (1, 2), (1, 3)):
+            mm(1, l, t, 0, S)
 
         ysb = {t: sb("ysb%d" % t, [P, S], F32) for t in range(1, PACK)}
         junk = sb("junk", [P, PACK, S], BF16)

@@ -123,8 +123,8 @@ def tile_picked_yadain_none_po_kernel(tc, x_words, x_scales, w1, offs, style, ou
         gather_words(0, 0, 0, S, sb("gw00", [P, S], I32))
         gather_words(0, 1, 0, S, sb("gw01", [P, S], I32))
         deal(0, 0, 0, 64, False)
-        deal(0, 64, 64, 100, False)
-        deal(0, 64, 100, P, True)
+        deal(0, 64, 64, 80, False)
+        deal(0, 64, 80, P, True)
         load_w(1, 0, 48, 0)
         load_w(1, 48, 96, 48)
         load_w(1, 96, P, 96)

@@ -106,6 +106,8 @@ def tile_picked_yadain_none_po_kernel(tc, x_words, x_scales, w1, offs, style, ou
 
         acc = [[psum.tile([P, S], F32, name="acc%d%d" % (l, t)) for t in range(PACK)] for l in range(2)]
 
+        opened = set()
+
         def mm(g, l, t, c0, c1):
             nc.tensor.matmul_mx(
                 out=acc[l][t][:, c0:c1],
@@ -113,9 +115,10 @@ def tile_picked_yadain_none_po_kernel(tc, x_words, x_scales, w1, offs, style, ou
                 lhsT_scale=ws[g][:, P * t:P * (t + 1)],
                 rhs=gw[g, l, c0][:].bitcast(FP8X4),
                 rhs_scale=planes[g][:, S * l + c0:S * l + c1],
-                start=(g == 0),
-                stop=(g == PASSES - 1 and c1 == S),
+                start=(l, t) not in opened,
+                stop=(l, t) in opened,
             )
+            opened.add((l, t))
 
         gather_scales(0)
         gather_scales(1)
@@ -128,15 +131,14 @@ def tile_picked_yadain_none_po_kernel(tc, x_words, x_scales, w1, offs, style, ou
         load_w(1, 0, 48, 0)
         load_w(1, 48, 96, 48)
         load_w(1, 96, P, 96)
-        quant_w(0, 0, 1)
         quant_w(0, 1, 2)
+        quant_w(0, 0, 1)
         quant_w(0, 2, PACK)
         planes.append(stage.tile([P, 2 * S], U8, name="plane1", align_bytes=64, offset=P * M_BYTES))
         nc.vector.memset(planes[1][:].bitcast(I32), 0)
         place_scales(1, nc.sync)
-        for l in range(2):
-            for t in range(PACK):
-                mm(0, l, t, 0, S)
+        for l, t in ((0, 1), (0, 0), (0, 2), (1, 0), (0, 3), (1, 1)):
+            mm(0, l, t, 0, S)
         gather_words(1, 0, 0, S, sb("gw10", [P, S], I32))
         gather_words(1, 1, 0, 512, sb("gw11a", [P, 512], I32))
         deal(1, 0, 0, 48, False)
@@ -145,8 +147,8 @@ def tile_picked_yadain_none_po_kernel(tc, x_words, x_scales, w1, offs, style, ou
         deal(1, 96, 122, P, False)
         for t in (1, 0, 2, 3):
             quant_w(1, t, t + 1)
-        for l, t in ((0, 1), (0, 0), (0, 2), (1, 0), (0, 3), (1, 1), (1, 2), (1, 3)):
-            mm(1, l, t, 0, S)
+        for g, l, t in ((1, 0, 1), (1, 0, 0), (1, 0, 2), (1, 1, 0), (1, 0, 3), (1, 1, 1), (1, 1, 2), (0, 1, 2), (1, 1, 3), (0, 1, 3)):
+            mm(g, l, t, 0, S)
 
         ysb = {t: sb("ysb%d" % t, [P, S], F32) for t in range(1, PACK)}
         junk = sb("junk", [P, PACK, S], BF16)

@@ -20,8 +20,15 @@ P = 128
 PACK = 4
 PASSES = K // (P * PACK)
 QUADS = 4
-ROWS = 16
-M_BYTES = PACK * PACK * 4
+SCALE_ROWS = 16
+PLACE_BYTES = PACK * PACK * 4
+HALF = P // 2
+Y, Z = 0, 1
+
+PIECE_1, PIECE_2 = 48, 96
+VECTOR_FROM_0 = 80
+VECTOR_TO_1 = 122
+SCALAR_WEAVES_FROM = 352
 
 
 def tile_picked_yadain_none_po_kernel(tc, x_words, x_scales, w1, offs, style, out_0, out_1, out_2):
@@ -34,15 +41,17 @@ def tile_picked_yadain_none_po_kernel(tc, x_words, x_scales, w1, offs, style, ou
         def sb(name, shape, dtype):
             return keep.tile(shape, dtype, name=name, align_bytes=64)
 
-        lists = [sb("offs_sb", [P, S // 16], U16), sb("style_sb", [P, S // 16], U16)]
-        xs = sb("xs", [P, T], U8)
-        xw = [sb("xw%d" % g, [P, T], I32) for g in range(PASSES)]
-        raw = {}
-        planes = [sb("plane0", [P, 2 * S], U8)]
-        picked = sb("picked", [P, 2 * S], U8)
+        def staged(name, shape, dtype, place):
+            return stage.tile(shape, dtype, name=name, align_bytes=64, offset=place * PLACE_BYTES)
 
-        nc.vector.memset(xs[32:64, :].bitcast(I32), 0)
-        nc.vector.memset(xs[64:P, :].bitcast(I32), 0)
+        lists = [sb("offs_sb", [P, S // 16], U16), sb("style_sb", [P, S // 16], U16)]
+        scale_table = sb("scale_table", [P, T], U8)
+        word_table = [sb("word_table%d" % g, [P, T], I32) for g in range(PASSES)]
+        planes = [sb("plane0", [P, 2 * S], U8)]
+        picked_scales = sb("picked_scales", [P, 2 * S], U8)
+
+        nc.vector.memset(scale_table[32:64, :].bitcast(I32), 0)
+        nc.vector.memset(scale_table[64:P, :].bitcast(I32), 0)
         nc.gpsimd.memset(planes[0][:].bitcast(I32), 0)
 
         ystat = sb("ystat", [P, PACK, 8], F32)
@@ -50,153 +59,151 @@ def tile_picked_yadain_none_po_kernel(tc, x_words, x_scales, w1, offs, style, ou
         one = sb("one", [P, 1], F32)
         nc.gpsimd.memset(one[:], 1.0)
         nc.gpsimd.memset(zstat[:], 0.0)
-        nc.gpsimd.memset(ystat[:, 1:4, 0:1], 1.0 / S)
-        nc.gpsimd.memset(ystat[:, 1:4, 2:3], -float(S))
+        nc.gpsimd.memset(ystat[:, 1:PACK, 0:1], 1.0 / S)
+        nc.gpsimd.memset(ystat[:, 1:PACK, 2:3], -float(S))
         nc.gpsimd.memset(ystat[:, 0, 0:3], 1.0)
-        nc.scalar.activation(ystat[:, 1:4, 1], one[:].to_broadcast([P, 3]), ACT.Abs_reciprocal_sqrt, scale=1.0 / (EPS * S * S) ** 2)
-        nc.scalar.activation(ystat[:, 0, 1:2], one[:], ACT.Copy, scale=EPS)
+        nc.scalar.activation(ystat[:, :, 1], one[:].to_broadcast([P, PACK]), ACT.Abs_reciprocal_sqrt, scale=1.0 / EPS ** 2)
 
-        def load_x(g):
-            nc.sync.dma_start(xw[g][:], x_words[g].rearrange("p n t -> p (n t)").bitcast(I32))
+        raw = {}
 
-        def load_w(g, m0, m1, place):
+        def load_words(g):
+            nc.sync.dma_start(word_table[g][:], x_words[g].rearrange("p n j -> p (n j)").bitcast(I32))
+
+        def load_weights(g, m0, m1, place):
             rows = w1[g * P * PACK:(g + 1) * P * PACK, :].rearrange("(p j) c -> p j c", j=PACK)
-            raw[g, m0] = stage.tile([P, PACK, PACK * (m1 - m0)], F32, name="raw%d_%d" % (g, m0), align_bytes=64, offset=place * M_BYTES)
+            raw[g, m0] = staged("raw%d_%d" % (g, m0), [P, PACK, PACK * (m1 - m0)], F32, place)
             nc.sync.dma_start(raw[g, m0][:], rows[:, :, PACK * m0:PACK * m1])
 
-        nc.sync.dma_start(lists[0][:], offs)
-        nc.sync.dma_start(lists[1][:], style)
-        nc.sync.dma_start(xs[0:PASSES * ROWS, :].bitcast(I32), x_scales.rearrange("g q n -> (g q) n").bitcast(I32))
-        load_x(0)
-        load_w(0, 0, 64, 96 - 64)
-        load_w(0, 64, P, 96)
-        load_x(1)
+        nc.sync.dma_start(lists[Y][:], offs)
+        nc.sync.dma_start(lists[Z][:], style)
+        nc.scalar.dma_start(scale_table[0:PASSES * SCALE_ROWS, :].bitcast(I32), x_scales.rearrange("g q n -> (g q) n").bitcast(I32))
+        load_words(0)
+        load_weights(0, 0, HALF, PIECE_2 - HALF)
+        load_weights(0, HALF, P, PIECE_2)
+        load_words(1)
 
-        gw = {}
-        wb = [sb("wb%d" % g, [P, PACK, P, PACK], BF16) for g in range(PASSES)]
-        wq = [sb("wq%d" % g, [P, N], U32) for g in range(PASSES)]
-        ws = [sb("ws%d" % g, [P, N], U8) for g in range(PASSES)]
+        picked_words = {}
+        dealt = [sb("dealt%d" % g, [P, PACK, P, PACK], BF16) for g in range(PASSES)]
+        w_words = [sb("w_words%d" % g, [P, N], U32) for g in range(PASSES)]
+        w_plane = [sb("w_plane%d" % g, [P, N], U8) for g in range(PASSES)]
 
-        def gather_words(g, l, c0, c1, tile):
-            gw[g, l, c0] = tile
-            nc.vector.tensor_copy(tile[:].bitcast(U32), xw[g][:].bitcast(U32).indirect(lists[l][:, c0 // 16:c1 // 16]))
+        def gather_words(g, l):
+            picked_words[g, l] = sb("picked_words%d%d" % (g, l), [P, S], I32)
+            nc.vector.tensor_copy(picked_words[g, l][:].bitcast(U32), word_table[g][:].bitcast(U32).indirect(lists[l][:]))
 
         def gather_scales(l):
-            nc.vector.tensor_copy(picked[:, S * l:S * (l + 1)], xs[:].indirect(lists[l][:]))
+            nc.vector.tensor_copy(picked_scales[:, S * l:S * (l + 1)], scale_table[:].indirect(lists[l][:]))
 
-        def place_scales(g, eng):
+        def move_scales(g, queue):
             for q in range(QUADS):
-                src = picked[ROWS * g + 4 * q:ROWS * g + 4 * q + 4, :]
-                eng.dma_start(planes[g][32 * q:32 * q + 4, :].bitcast(I32), src.bitcast(I32))
+                src = picked_scales[SCALE_ROWS * g + 4 * q:SCALE_ROWS * g + 4 * q + 4, :]
+                queue.dma_start(planes[g][32 * q:32 * q + 4, :].bitcast(I32), src.bitcast(I32))
 
-        def deal(g, base, m0, m1, on_vector):
-            dst = wb[g][:, :, m0:m1, :].rearrange("p t m j -> p m j t")
-            src = raw[g, base][:, :, PACK * (m0 - base):PACK * (m1 - base)].rearrange("p j (m t) -> p m j t", t=PACK)
-            if on_vector:
-                nc.vector.tensor_copy(dst, src)
-            else:
-                nc.scalar.copy(dst, src)
+        def deal(copy, g, piece, m0, m1):
+            dst = dealt[g][:, :, m0:m1, :].rearrange("p t m j -> p m j t")
+            src = raw[g, piece][:, :, PACK * (m0 - piece):PACK * (m1 - piece)].rearrange("p j (m t) -> p m j t", t=PACK)
+            copy(dst, src)
 
-        def quant_w(g, t0, t1):
+        def quantise_weights(g, c0, c1):
             nc.vector.quantize_mx(
-                out=wq[g][:, P * t0:P * t1].bitcast(FP8X4),
-                scales=ws[g][:, P * t0:P * t1],
-                in_=wb[g][:, t0:t1].rearrange("p t m j -> p (t m j)"),
+                out=w_words[g][:, c0:c1].bitcast(FP8X4),
+                scales=w_plane[g][:, c0:c1],
+                in_=dealt[g][:].rearrange("p t m j -> p (t m j)")[:, PACK * c0:PACK * c1],
             )
 
-        acc = [[psum.tile([P, S], F32, name="acc%d%d" % (l, t)) for t in range(PACK)] for l in range(2)]
+        acc = [[psum.tile([P, S], F32, name="acc%d%d" % (l, t)) for t in range(PACK)] for l in (Y, Z)]
 
-        opened = set()
-
-        def mm(g, l, t, c0, c1):
+        def multiply(g, l, t, first):
             nc.tensor.matmul_mx(
-                out=acc[l][t][:, c0:c1],
-                lhsT=wq[g][:, P * t:P * (t + 1)].bitcast(FP8X4),
-                lhsT_scale=ws[g][:, P * t:P * (t + 1)],
-                rhs=gw[g, l, c0][:].bitcast(FP8X4),
-                rhs_scale=planes[g][:, S * l + c0:S * l + c1],
-                start=(l, t) not in opened,
-                stop=(l, t) in opened,
+                out=acc[l][t][:],
+                lhsT=w_words[g][:, P * t:P * (t + 1)].bitcast(FP8X4),
+                lhsT_scale=w_plane[g][:, P * t:P * (t + 1)],
+                rhs=picked_words[g, l][:].bitcast(FP8X4),
+                rhs_scale=planes[g][:, S * l:S * (l + 1)],
+                start=first,
+                stop=not first,
             )
-            opened.add((l, t))
 
-        gather_scales(0)
-        gather_scales(1)
-        place_scales(0, nc.scalar)
-        gather_words(0, 0, 0, S, sb("gw00", [P, S], I32))
-        gather_words(0, 1, 0, S, sb("gw01", [P, S], I32))
-        deal(0, 0, 0, 64, False)
-        deal(0, 64, 64, 80, False)
-        deal(0, 64, 80, P, True)
-        load_w(1, 0, 48, 0)
-        load_w(1, 48, 96, 48)
-        load_w(1, 96, P, 96)
-        quant_w(0, 1, 2)
-        quant_w(0, 0, 1)
-        quant_w(0, 2, PACK)
-        planes.append(stage.tile([P, 2 * S], U8, name="plane1", align_bytes=64, offset=P * M_BYTES))
+        early_banks = ((Y, 1), (Y, 0), (Y, 2), (Z, 0), (Y, 3), (Z, 1))
+        late_banks = ((Z, 2), (Z, 3))
+
+        gather_scales(Y)
+        gather_scales(Z)
+        move_scales(0, nc.scalar)
+        gather_words(0, Y)
+        gather_words(0, Z)
+        deal(nc.scalar.copy, 0, 0, 0, HALF)
+        deal(nc.scalar.copy, 0, HALF, HALF, VECTOR_FROM_0)
+        deal(nc.vector.tensor_copy, 0, HALF, VECTOR_FROM_0, P)
+        load_weights(1, 0, PIECE_1, 0)
+        load_weights(1, PIECE_1, PIECE_2, PIECE_1)
+        load_weights(1, PIECE_2, P, PIECE_2)
+        quantise_weights(0, P, 2 * P)
+        quantise_weights(0, 0, P)
+        quantise_weights(0, 2 * P, N)
+        planes.append(staged("plane1", [P, 2 * S], U8, P))
         nc.vector.memset(planes[1][:].bitcast(I32), 0)
-        place_scales(1, nc.sync)
-        for l, t in ((0, 1), (0, 0), (0, 2), (1, 0), (0, 3), (1, 1)):
-            mm(0, l, t, 0, S)
-        gather_words(1, 0, 0, S, sb("gw10", [P, S], I32))
-        gather_words(1, 1, 0, 512, sb("gw11a", [P, 512], I32))
-        deal(1, 0, 0, 48, False)
-        deal(1, 48, 48, 96, False)
-        deal(1, 96, 96, 122, True)
-        deal(1, 96, 122, P, False)
-        for t in (1, 0, 2, 3):
-            quant_w(1, t, t + 1)
-        for g, l, t in ((1, 0, 1), (1, 0, 0), (1, 0, 2), (1, 1, 0), (1, 0, 3), (1, 1, 1), (1, 1, 2), (0, 1, 2), (1, 1, 3), (0, 1, 3)):
-            mm(g, l, t, 0, S)
+        move_scales(1, nc.sync)
+        for l, t in early_banks:
+            multiply(0, l, t, True)
 
-        ysb = {t: sb("ysb%d" % t, [P, S], F32) for t in range(1, PACK)}
-        junk = sb("junk", [P, PACK, S], BF16)
-        m2y = sb("m2y", [P, PACK], F32)
-        st = [[sb("st%d%d" % (l, t), [P, 6], F32) for t in range(PACK)] for l in range(2)]
+        gather_words(1, Y)
+        gather_words(1, Z)
+        deal(nc.scalar.copy, 1, 0, 0, PIECE_1)
+        deal(nc.scalar.copy, 1, PIECE_1, PIECE_1, PIECE_2)
+        deal(nc.vector.tensor_copy, 1, PIECE_2, PIECE_2, VECTOR_TO_1)
+        deal(nc.scalar.copy, 1, PIECE_2, VECTOR_TO_1, P)
+        for t in (1, 0):
+            quantise_weights(1, P * t, P * t + HALF)
+        for t in (1, 0):
+            quantise_weights(1, P * t + HALF, P * (t + 1))
+        for t in (2, 3):
+            quantise_weights(1, P * t, P * (t + 1))
+        for l, t in early_banks:
+            multiply(1, l, t, False)
+        for l, t in late_banks:
+            multiply(1, l, t, True)
+            multiply(0, l, t, False)
+
+        y_copy = {t: sb("y_copy%d" % t, [P, S], F32) for t in range(1, PACK)}
+        squares = sb("squares", [P, PACK, S], BF16)
+        sum_sq = sb("sum_sq", [P, PACK], F32)
+        tuples = [[sb("tuples%d%d" % (l, t), [P, 6], F32) for t in range(PACK)] for l in (Y, Z)]
         prod = sb("prod", [P, PACK, 4], F32)
-        inv = [sb("inv%d" % t, [P, 1], F32) for t in range(PACK)]
+        root = [sb("root%d" % t, [P, 1], F32) for t in range(PACK)]
         gain = [sb("gain%d" % t, [P, 2], F32) for t in range(PACK)]
-        shift = sb("shift", [P, 1], F32)
+        shift_0 = sb("shift_0", [P, 1], F32)
         res = sb("res", [P, PACK, S], F32)
         out_rows = out_0.rearrange("(p t) c -> p t c", t=PACK)
 
         def first_read(t):
-            nc.scalar.activation(ysb[t][:], acc[0][t][:], ACT.Copy, scale=-1.0, accum_out=ystat[:, t, 3:4])
+            nc.scalar.activation(y_copy[t][:], acc[Y][t][:], ACT.Copy, scale=-1.0 / S, accum_out=ystat[:, t, 3:4])
 
         def second_read(t):
-            nc.scalar.activation(junk[:, t, :], acc[0][t][:], ACT.Square, scale=float(S), bias=ystat[:, t, 3:4], accum_out=m2y[:, t:t + 1])
+            nc.scalar.activation(squares[:, t, :], acc[Y][t][:], ACT.Square, bias=ystat[:, t, 3:4], accum_out=sum_sq[:, t:t + 1])
 
-        def stats(l, t):
-            nc.vector.bn_stats(st[l][t][:], acc[l][t][:])
+        def bn_read(l, t):
+            nc.vector.bn_stats(tuples[l][t][:], acc[l][t][:])
 
-        def aggr(l, t):
-            nc.vector.bn_aggr(zstat[:, t, 1:3] if l else ystat[:, t, 3:5], st[l][t][:])
+        def bn_join(l, t):
+            nc.vector.bn_aggr(zstat[:, t, 1:3] if l == Z else ystat[:, t, 3:5], tuples[l][t][:])
 
         def products(t0, t1):
-            spread = zstat[:, t0:t1, 2:3].to_broadcast([P, t1 - t0, 4])
-            nc.vector.scalar_tensor_tensor(prod[:, t0:t1, :], spread, EPS, ystat[:, t0:t1, 0:4], ALU.add, ALU.mult)
+            var_z = zstat[:, t0:t1, 2:3].to_broadcast([P, t1 - t0, 4])
+            nc.vector.scalar_tensor_tensor(prod[:, t0:t1, :], var_z, EPS, ystat[:, t0:t1, 0:4], ALU.add, ALU.mult)
 
-        def root(t):
-            spread = m2y[:, t:t + 1] if t else ystat[:, t, 4:5]
-            nc.scalar.activation(inv[t][:], spread, ACT.Abs_reciprocal_sqrt, scale=prod[:, t, 0:1], bias=prod[:, t, 1:2])
+        def inverse_root(t):
+            spread_y = sum_sq[:, t:t + 1] if t else ystat[:, t, 4:5]
+            nc.scalar.activation(root[t][:], spread_y, ACT.Abs_reciprocal_sqrt, scale=prod[:, t, 0:1], bias=prod[:, t, 1:2])
 
         def gains(t):
-            nc.vector.scalar_tensor_tensor(gain[t][:], prod[:, t, 2:4], inv[t][:], zstat[:, t, 0:2], ALU.mult, ALU.add if t else ALU.subtract)
+            nc.vector.scalar_tensor_tensor(gain[t][:], prod[:, t, 2:4], root[t][:], zstat[:, t, 0:2], ALU.mult, ALU.add if t else ALU.subtract)
 
-        def store(t0, t1):
-            nc.sync.dma_start(out_rows[:, t0:t1, :], res[:, t0:t1, :])
+        def affine(t):
+            nc.vector.tensor_scalar(res[:, t, :], y_copy[t][:], gain[t][:, 0:1], gain[t][:, 1:2], ALU.mult, ALU.add)
 
-        def affine(t, eng):
-            if eng is nc.scalar:
-                eng.activation(res[:, t, :], ysb[t][:], ACT.Identity, scale=gain[t][:, 0:1], bias=gain[t][:, 1:2])
-            else:
-                eng.tensor_scalar(res[:, t, :], ysb[t][:], gain[t][:, 0:1], gain[t][:, 1:2], ALU.mult, ALU.add)
-
-        def affine_psum(t):
-            nc.scalar.activation(shift[:], gain[t][:, 1:2], ACT.Copy, scale=-1.0)
-            nc.scalar.activation(res[:, t, :], acc[0][t][:], ACT.Identity, scale=gain[t][:, 0:1], bias=shift[:])
-            store(t, t + 1)
+        def store(tiles):
+            nc.sync.dma_start(out_rows[:, tiles, :], res[:, tiles, :])
 
         first_read(1)
         first_read(2)
@@ -204,59 +211,53 @@ def tile_picked_yadain_none_po_kernel(tc, x_words, x_scales, w1, offs, style, ou
         first_read(3)
         second_read(2)
         second_read(3)
-        stats(0, 0)
-        stats(1, 0)
-        aggr(0, 0)
-        stats(1, 1)
-        aggr(1, 0)
-        stats(1, 2)
-        aggr(1, 1)
+        bn_read(Y, 0)
+        bn_read(Z, 0)
+        bn_join(Y, 0)
+        bn_read(Z, 1)
+        bn_join(Z, 0)
+        bn_read(Z, 2)
+        bn_join(Z, 1)
         products(0, 2)
-        root(1)
-        root(0)
-        stats(1, 3)
-        aggr(1, 2)
+        inverse_root(1)
+        inverse_root(0)
+        bn_read(Z, 3)
+        bn_join(Z, 2)
         gains(1)
         products(2, 3)
-        aggr(1, 3)
-        root(2)
+        bn_join(Z, 3)
+        inverse_root(2)
         gains(0)
-        products(3, 4)
-        root(3)
+        products(3, PACK)
+        inverse_root(3)
         gains(2)
-        affine(1, nc.vector)
-        store(1, 2)
+        affine(1)
+        store(slice(1, 2))
         gains(3)
-        affine_psum(0)
-        affine(2, nc.vector)
-        affine(3, nc.vector)
-        store(2, PACK)
+        nc.scalar.activation(shift_0[:], gain[0][:, 1:2], ACT.Copy, scale=-1.0)
+        nc.scalar.activation(res[:, 0, :], acc[Y][0][:], ACT.Identity, scale=gain[0][:, 0:1], bias=shift_0[:])
+        affine(2)
+        store(slice(2, 3))
+        affine(3)
+        store(slice(0, PACK, 3))
 
-        rb = [sb("rb%d" % h, [P, S // 2, PACK], BF16) for h in range(2)]
-        oq = sb("oq", [P, S], U32)
-        osc = sb("osc", [P, S], U8)
+        woven = [sb("woven%d" % h, [P, S // 2, PACK], BF16) for h in range(2)]
+        out_words = sb("out_words", [P, S], U32)
+        out_plane = sb("out_plane", [P, S], U8)
+        words_dram = out_1[0].rearrange("p n t -> p (n t)").bitcast(I32)
 
-        def weave(c0, c1, on_vector):
-            dst = rb[c0 // 256][:, c0 % 256:(c1 - 1) % 256 + 1, :].rearrange("p (c i) t -> p c t i", i=4)
+        def weave(copy, h, c0, c1):
+            dst = woven[h][:, c0 - h * S // 2:c1 - h * S // 2, :].rearrange("p (c i) t -> p c t i", i=4)
             src = res[:, :, c0:c1].rearrange("p t (c i) -> p c t i", i=4)
-            if on_vector:
-                nc.vector.tensor_copy(dst, src)
-            else:
-                nc.scalar.copy(dst, src)
+            copy(dst, src)
 
-        def quant_out(c0, c1):
-            nc.vector.quantize_mx(
-                out=oq[:, c0:c1].bitcast(FP8X4),
-                scales=osc[:, c0:c1],
-                in_=rb[c0 // 256][:].rearrange("p c t -> p (c t)"),
-            )
-
-        weave(0, 256, True)
-        weave(352, S, False)
-        weave(256, 352, True)
-        quant_out(0, 256)
-        quant_out(256, S)
-        nc.sync.dma_start(out_1[0].rearrange("p n t -> p (n t)").bitcast(I32), oq[:].bitcast(I32))
+        weave(nc.vector.tensor_copy, 0, 0, S // 2)
+        weave(nc.scalar.copy, 1, SCALAR_WEAVES_FROM, S)
+        weave(nc.vector.tensor_copy, 1, S // 2, SCALAR_WEAVES_FROM)
+        for h in range(2):
+            cols = slice(h * S // 2, (h + 1) * S // 2)
+            nc.vector.quantize_mx(out=out_words[:, cols].bitcast(FP8X4), scales=out_plane[:, cols], in_=woven[h][:].rearrange("p c t -> p (c t)"))
+            nc.sync.dma_start(words_dram[:, cols], out_words[:, cols].bitcast(I32))
         for q in range(QUADS):
-            eng = nc.scalar if q % 2 else nc.sync
-            eng.dma_start(out_2[0, 4 * q:4 * q + 4, :].bitcast(I32), osc[32 * q:32 * q + 4, :].bitcast(I32))
+            queue = nc.scalar if q % 2 else nc.sync
+            queue.dma_start(out_2[0, 4 * q:4 * q + 4, :].bitcast(I32), out_plane[32 * q:32 * q + 4, :].bitcast(I32))

@@ -76,7 +76,7 @@ def tile_picked_yadain_none_po_kernel(tc, x_words, x_scales, w1, offs, style, ou
 
         nc.sync.dma_start(lists[Y][:], offs)
         nc.sync.dma_start(lists[Z][:], style)
-        nc.scalar.dma_start(scale_table[0:PASSES * SCALE_ROWS, :].bitcast(I32), x_scales.rearrange("g q n -> (g q) n").bitcast(I32))
+        nc.sync.dma_start(scale_table[0:PASSES * SCALE_ROWS, :].bitcast(I32), x_scales.rearrange("g q n -> (g q) n").bitcast(I32))
         load_words(0)
         load_weights(0, 0, HALF, PIECE_2 - HALF)
         load_weights(0, HALF, P, PIECE_2)
@@ -257,7 +257,7 @@ def tile_picked_yadain_none_po_kernel(tc, x_words, x_scales, w1, offs, style, ou
         for h in range(2):
             cols = slice(h * S // 2, (h + 1) * S // 2)
             nc.vector.quantize_mx(out=out_words[:, cols].bitcast(FP8X4), scales=out_plane[:, cols], in_=woven[h][:].rearrange("p c t -> p (c t)"))
-            nc.sync.dma_start(words_dram[:, cols], out_words[:, cols].bitcast(I32))
+        nc.sync.dma_start(words_dram, out_words[:].bitcast(I32))
         for q in range(QUADS):
             queue = nc.scalar if q % 2 else nc.sync
             queue.dma_start(out_2[0, 4 * q:4 * q + 4, :].bitcast(I32), out_plane[32 * q:32 * q + 4, :].bitcast(I32))

@@ -74,9 +74,9 @@ def tile_picked_yadain_none_po_kernel(tc, x_words, x_scales, w1, offs, style, ou
             raw[g, m0] = staged("raw%d_%d" % (g, m0), [P, PACK, PACK * (m1 - m0)], F32, place)
             nc.sync.dma_start(raw[g, m0][:], rows[:, :, PACK * m0:PACK * m1])
 
+        nc.sync.dma_start(scale_table[0:PASSES * SCALE_ROWS, :].bitcast(I32), x_scales.rearrange("g q n -> (g q) n").bitcast(I32))
         nc.sync.dma_start(lists[Y][:], offs)
         nc.sync.dma_start(lists[Z][:], style)
-        nc.sync.dma_start(scale_table[0:PASSES * SCALE_ROWS, :].bitcast(I32), x_scales.rearrange("g q n -> (g q) n").bitcast(I32))
         load_words(0)
         load_weights(0, 0, HALF, PIECE_2 - HALF)
         load_weights(0, HALF, P, PIECE_2)

@@ -39,10 +39,10 @@ def tile_picked_yadain_none_po_kernel(tc, x_words, x_scales, w1, offs, style, ou
         psum = ctx.enter_context(tc.psum_pool(name="psum", bufs=1))
 
         def sb(name, shape, dtype):
-            return keep.tile(shape, dtype, name=name, align_bytes=64)
+            return keep.tile(shape, dtype, name=name, align_bytes=256)
 
         def staged(name, shape, dtype, place):
-            return stage.tile(shape, dtype, name=name, align_bytes=64, offset=place * PLACE_BYTES)
+            return stage.tile(shape, dtype, name=name, align_bytes=256, offset=place * PLACE_BYTES)
 
         lists = [sb("offs_sb", [P, S // 16], U16), sb("style_sb", [P, S // 16], U16)]
         scale_table = sb("scale_table", [P, T], U8)

@@ -24,6 +24,7 @@ SCALE_ROWS = 16
 PLACE_BYTES = PACK * PACK * 4
 HALF = P // 2
 Y, Z = 0, 1
+ROW = (2, 0, 1, 3)
 
 PIECE_1, PIECE_2 = 48, 96
 VECTOR_FROM_0 = 80
@@ -38,17 +39,17 @@ def tile_picked_yadain_none_po_kernel(tc, x_words, x_scales, w1, offs, style, ou
         stage = ctx.enter_context(tc.tile_pool(name="stage", bufs=1))
         psum = ctx.enter_context(tc.psum_pool(name="psum", bufs=1))
 
-        def sb(name, shape, dtype):
-            return keep.tile(shape, dtype, name=name, align_bytes=256)
+        def sb(name, shape, dtype, align=256):
+            return keep.tile(shape, dtype, name=name, align_bytes=align)
 
         def staged(name, shape, dtype, place):
-            return stage.tile(shape, dtype, name=name, align_bytes=256, offset=place * PLACE_BYTES)
+            return stage.tile(shape, dtype, name=name, align_bytes=1024 if place else 4096, offset=place * PLACE_BYTES)
 
         lists = [sb("offs_sb", [P, S // 16], U16), sb("style_sb", [P, S // 16], U16)]
-        scale_table = sb("scale_table", [P, T], U8)
-        word_table = [sb("word_table%d" % g, [P, T], I32) for g in range(PASSES)]
-        planes = [sb("plane0", [P, 2 * S], U8)]
-        picked_scales = sb("picked_scales", [P, 2 * S], U8)
+        scale_table = sb("scale_table", [P, T], U8, 2048)
+        word_table = [sb("word_table%d" % g, [P, T], I32, 4096) for g in range(PASSES)]
+        planes = [sb("plane0", [P, 2 * S], U8, 1024)]
+        picked_scales = sb("picked_scales", [P, 2 * S], U8, 1024)
 
         nc.vector.memset(scale_table[32:64, :].bitcast(I32), 0)
         nc.vector.memset(scale_table[64:P, :].bitcast(I32), 0)
@@ -116,8 +117,8 @@ def tile_picked_yadain_none_po_kernel(tc, x_words, x_scales, w1, offs, style, ou
         def multiply(g, l, t, first):
             nc.tensor.matmul_mx(
                 out=acc[l][t][:],
-                lhsT=w_words[g][:, P * t:P * (t + 1)].bitcast(FP8X4),
-                lhsT_scale=w_plane[g][:, P * t:P * (t + 1)],
+                lhsT=w_words[g][:, P * ROW[t]:P * (ROW[t] + 1)].bitcast(FP8X4),
+                lhsT_scale=w_plane[g][:, P * ROW[t]:P * (ROW[t] + 1)],
                 rhs=picked_words[g, l][:].bitcast(FP8X4),
                 rhs_scale=planes[g][:, S * l:S * (l + 1)],
                 start=first,
@@ -138,9 +139,9 @@ def tile_picked_yadain_none_po_kernel(tc, x_words, x_scales, w1, offs, style, ou
         load_weights(1, 0, PIECE_1, 0)
         load_weights(1, PIECE_1, PIECE_2, PIECE_1)
         load_weights(1, PIECE_2, P, PIECE_2)
-        quantise_weights(0, P, 2 * P)
         quantise_weights(0, 0, P)
-        quantise_weights(0, 2 * P, N)
+        quantise_weights(0, P, 3 * P)
+        quantise_weights(0, 3 * P, N)
         planes.append(staged("plane1", [P, 2 * S], U8, P))
         nc.vector.memset(planes[1][:].bitcast(I32), 0)
         move_scales(1, nc.sync)
@@ -154,11 +155,11 @@ def tile_picked_yadain_none_po_kernel(tc, x_words, x_scales, w1, offs, style, ou
         deal(nc.vector.tensor_copy, 1, PIECE_2, PIECE_2, VECTOR_TO_1)
         deal(nc.scalar.copy, 1, PIECE_2, VECTOR_TO_1, P)
         for t in (1, 0):
-            quantise_weights(1, P * t, P * t + HALF)
+            quantise_weights(1, P * ROW[t], P * ROW[t] + HALF)
         for t in (1, 0):
-            quantise_weights(1, P * t + HALF, P * (t + 1))
+            quantise_weights(1, P * ROW[t] + HALF, P * (ROW[t] + 1))
         for t in (2, 3):
-            quantise_weights(1, P * t, P * (t + 1))
+            quantise_weights(1, P * ROW[t], P * (ROW[t] + 1))
         for l, t in early_banks:
             multiply(1, l, t, False)
         for l, t in late_banks:
@@ -173,7 +174,7 @@ def tile_picked_yadain_none_po_kernel(tc, x_words, x_scales, w1, offs, style, ou
         root = [sb("root%d" % t, [P, 1], F32) for t in range(PACK)]
         gain = [sb("gain%d" % t, [P, 2], F32) for t in range(PACK)]
         shift_0 = sb("shift_0", [P, 1], F32)
-        res = sb("res", [P, PACK, S], F32)
+        res = sb("res", [P, PACK, S], F32, 4096)
         out_rows = out_0.rearrange("(p t) c -> p t c", t=PACK)
 
         def first_read(t):
@@ -200,7 +201,7 @@ def tile_picked_yadain_none_po_kernel(tc, x_words, x_scales, w1, offs, style, ou
             nc.vector.scalar_tensor_tensor(gain[t][:], prod[:, t, 2:4], root[t][:], zstat[:, t, 0:2], ALU.mult, ALU.add if t else ALU.subtract)
 
         def affine(t):
-            nc.vector.tensor_scalar(res[:, t, :], y_copy[t][:], gain[t][:, 0:1], gain[t][:, 1:2], ALU.mult, ALU.add)
+            nc.vector.tensor_scalar(res[:, ROW[t], :], y_copy[t][:], gain[t][:, 0:1], gain[t][:, 1:2], ALU.mult, ALU.add)
 
         def store(tiles):
             nc.sync.dma_start(out_rows[:, tiles, :], res[:, tiles, :])
@@ -232,18 +233,18 @@ def tile_picked_yadain_none_po_kernel(tc, x_words, x_scales, w1, offs, style, ou
         inverse_root(3)
         gains(2)
         affine(1)
-        store(slice(1, 2))
+        store(slice(0, 1))
         gains(3)
         nc.scalar.activation(shift_0[:], gain[0][:, 1:2], ACT.Copy, scale=-1.0)
-        nc.scalar.activation(res[:, 0, :], acc[Y][0][:], ACT.Identity, scale=gain[0][:, 0:1], bias=shift_0[:])
+        nc.scalar.activation(res[:, ROW[0], :], acc[Y][0][:], ACT.Identity, scale=gain[0][:, 0:1], bias=shift_0[:])
         affine(2)
-        store(slice(2, 3))
+        store(slice(1, 2))
         affine(3)
-        store(slice(0, PACK, 3))
+        store(slice(2, PACK))
 
         woven = [sb("woven%d" % h, [P, S // 2, PACK], BF16) for h in range(2)]
-        out_words = sb("out_words", [P, S], U32)
-        out_plane = sb("out_plane", [P, S], U8)
+        out_words = sb("out_words", [P, S], U32, 2048)
+        out_plane = sb("out_plane", [P, S], U8, 512)
         words_dram = out_1[0].rearrange("p n t -> p (n t)").bitcast(I32)
 
         def weave(copy, h, c0, c1):

@@ -101,8 +101,8 @@ def tile_picked_yadain_none_po_kernel(tc, x_words, x_scales, w1, offs, style, ou
                 queue.dma_start(planes[g][32 * q:32 * q + 4, :].bitcast(I32), src.bitcast(I32))
 
         def deal(copy, g, piece, m0, m1):
-            dst = dealt[g][:, :, m0:m1, :].rearrange("p t m j -> p m j t")
-            src = raw[g, piece][:, :, PACK * (m0 - piece):PACK * (m1 - piece)].rearrange("p j (m t) -> p m j t", t=PACK)
+            dst = dealt[g][:, :, m0:m1, :].rearrange("p (u v) m j -> p m u j v", v=2)
+            src = raw[g, piece][:, :, PACK * (m0 - piece):PACK * (m1 - piece)].rearrange("p j (m u v) -> p m u j v", u=2, v=2)
             copy(dst, src)
 
         def quantise_weights(g, c0, c1):

@@ -130,7 +130,7 @@ def tile_picked_yadain_none_po_kernel(tc, x_words, x_scales, w1, offs, style, ou
 
         gather_scales(Y)
         gather_scales(Z)
-        move_scales(0, nc.scalar)
+        move_scales(0, nc.sync)
         gather_words(0, Y)
         gather_words(0, Z)
         deal(nc.scalar.copy, 0, 0, 0, HALF)
@@ -145,6 +145,16 @@ def tile_picked_yadain_none_po_kernel(tc, x_words, x_scales, w1, offs, style, ou
         planes.append(staged("plane1", [P, 2 * S], U8, P))
         nc.vector.memset(planes[1][:].bitcast(I32), 0)
         move_scales(1, nc.sync)
+        for (l, t), columns in zip(early_banks, (S, S // 2)):
+            nc.tensor.matmul_mx(
+                out=acc[l][t][:, 0:columns],
+                lhsT=w_words[0][:, 0:P].bitcast(FP8X4),
+                lhsT_scale=w_plane[0][:, 0:P],
+                rhs=w_words[0][:, 0:columns].bitcast(FP8X4),
+                rhs_scale=w_plane[0][:, 0:columns],
+                start=True,
+                stop=True,
+            )
         for l, t in early_banks:
             multiply(0, l, t, True)
 

@@ -23,6 +23,8 @@ QUADS = 4
 SCALE_ROWS = 16
 PLACE_BYTES = PACK * PACK * 4
 HALF = P // 2
+TABLE_ROW = P - PASSES * SCALE_ROWS
+PLANE_0 = P + HALF // 2
 Y, Z = 0, 1
 ROW = (2, 0, 1, 3)
 
@@ -48,22 +50,19 @@ def tile_picked_yadain_none_po_kernel(tc, x_words, x_scales, w1, offs, style, ou
         lists = [sb("offs_sb", [P, S // 16], U16), sb("style_sb", [P, S // 16], U16)]
         scale_table = sb("scale_table", [P, T], U8, 2048)
         word_table = [sb("word_table%d" % g, [P, T], I32, 4096) for g in range(PASSES)]
-        planes = [sb("plane0", [P, 2 * S], U8, 1024)]
+        one = staged("one", [P, 1], F32, PLANE_0)
+        planes = [staged("plane0", [P, 2 * S], U8, PLANE_0)]
         picked_scales = sb("picked_scales", [P, 2 * S], U8, 1024)
 
-        nc.vector.memset(scale_table[32:64, :].bitcast(I32), 0)
-        nc.vector.memset(scale_table[64:P, :].bitcast(I32), 0)
-        nc.gpsimd.memset(planes[0][:].bitcast(I32), 0)
+        nc.vector.memset(scale_table[0:TABLE_ROW, :].bitcast(I32), 0)
 
         ystat = sb("ystat", [P, PACK, 8], F32)
         zstat = sb("zstat", [P, PACK, 8], F32)
-        one = sb("one", [P, 1], F32)
         nc.gpsimd.memset(one[:], 1.0)
-        nc.gpsimd.memset(zstat[:], 0.0)
-        nc.gpsimd.memset(ystat[:, 1:PACK, 0:1], 1.0 / S)
-        nc.gpsimd.memset(ystat[:, 1:PACK, 2:3], -float(S))
-        nc.gpsimd.memset(ystat[:, 0, 0:3], 1.0)
         nc.scalar.activation(ystat[:, :, 1], one[:].to_broadcast([P, PACK]), ACT.Abs_reciprocal_sqrt, scale=1.0 / EPS ** 2)
+        for column, value in ((zstat[:, :, 0], 0.0), (ystat[:, 1:PACK, 0], 1.0 / S), (ystat[:, 1:PACK, 2], -float(S)), (ystat[:, 0, 0:3:2], 1.0)):
+            nc.scalar.activation(column, one[:].to_broadcast(list(column.shape)), ACT.Copy, scale=value)
+        nc.gpsimd.memset(planes[0][:].bitcast(I32), 0)
 
         raw = {}
 
@@ -75,7 +74,7 @@ def tile_picked_yadain_none_po_kernel(tc, x_words, x_scales, w1, offs, style, ou
             raw[g, m0] = staged("raw%d_%d" % (g, m0), [P, PACK, PACK * (m1 - m0)], F32, place)
             nc.sync.dma_start(raw[g, m0][:], rows[:, :, PACK * m0:PACK * m1])
 
-        nc.sync.dma_start(scale_table[0:PASSES * SCALE_ROWS, :].bitcast(I32), x_scales.rearrange("g q n -> (g q) n").bitcast(I32))
+        nc.sync.dma_start(scale_table[TABLE_ROW:P, :].bitcast(I32), x_scales.rearrange("g q n -> (g q) n").bitcast(I32))
         nc.sync.dma_start(lists[Y][:], offs)
         nc.sync.dma_start(lists[Z][:], style)
         load_words(0)
@@ -97,7 +96,7 @@ def tile_picked_yadain_none_po_kernel(tc, x_words, x_scales, w1, offs, style, ou
 
         def move_scales(g, queue):
             for q in range(QUADS):
-                src = picked_scales[SCALE_ROWS * g + 4 * q:SCALE_ROWS * g + 4 * q + 4, :]
+                src = picked_scales[TABLE_ROW + SCALE_ROWS * g + 4 * q:TABLE_ROW + SCALE_ROWS * g + 4 * q + 4, :]
                 queue.dma_start(planes[g][32 * q:32 * q + 4, :].bitcast(I32), src.bitcast(I32))
 
         def deal(copy, g, piece, m0, m1):

@@ -24,7 +24,6 @@ SCALE_ROWS = 16
 PLACE_BYTES = PACK * PACK * 4
 HALF = P // 2
 TABLE_ROW = P - PASSES * SCALE_ROWS
-PLANE_0 = P + HALF // 2
 Y, Z = 0, 1
 ROW = (2, 0, 1, 3)
 
@@ -48,21 +47,23 @@ def tile_picked_yadain_none_po_kernel(tc, x_words, x_scales, w1, offs, style, ou
             return stage.tile(shape, dtype, name=name, align_bytes=1024 if place else 4096, offset=place * PLACE_BYTES)
 
         lists = [sb("offs_sb", [P, S // 16], U16), sb("style_sb", [P, S // 16], U16)]
+        plane_1 = sb("plane1", [P, 2 * S], U8, 1024)
         scale_table = sb("scale_table", [P, T], U8, 2048)
         word_table = [sb("word_table%d" % g, [P, T], I32, 4096) for g in range(PASSES)]
-        one = staged("one", [P, 1], F32, PLANE_0)
-        planes = [staged("plane0", [P, 2 * S], U8, PLANE_0)]
+        planes = [sb("plane0", [P, 2 * S], U8, 1024), plane_1]
         picked_scales = sb("picked_scales", [P, 2 * S], U8, 1024)
 
         nc.vector.memset(scale_table[0:TABLE_ROW, :].bitcast(I32), 0)
+        for g in range(PASSES):
+            nc.vector.memset(planes[g][:].bitcast(I32), 0)
 
         ystat = sb("ystat", [P, PACK, 8], F32)
         zstat = sb("zstat", [P, PACK, 8], F32)
+        one = sb("one", [P, 1], F32)
         nc.gpsimd.memset(one[:], 1.0)
         nc.scalar.activation(ystat[:, :, 1], one[:].to_broadcast([P, PACK]), ACT.Abs_reciprocal_sqrt, scale=1.0 / EPS ** 2)
         for column, value in ((zstat[:, :, 0], 0.0), (ystat[:, 1:PACK, 0], 1.0 / S), (ystat[:, 1:PACK, 2], -float(S)), (ystat[:, 0, 0:3:2], 1.0)):
             nc.scalar.activation(column, one[:].to_broadcast(list(column.shape)), ACT.Copy, scale=value)
-        nc.gpsimd.memset(planes[0][:].bitcast(I32), 0)
 
         raw = {}
 
@@ -141,8 +142,6 @@ def tile_picked_yadain_none_po_kernel(tc, x_words, x_scales, w1, offs, style, ou
         quantise_weights(0, 0, P)
         quantise_weights(0, P, 3 * P)
         quantise_weights(0, 3 * P, N)
-        planes.append(staged("plane1", [P, 2 * S], U8, P))
-        nc.vector.memset(planes[1][:].bitcast(I32), 0)
         move_scales(1, nc.sync)
         for (l, t), columns in zip(early_banks, (S, S // 2)):
             nc.tensor.matmul_mx(

@@ -125,12 +125,12 @@ def tile_picked_yadain_none_po_kernel(tc, x_words, x_scales, w1, offs, style, ou
                 stop=not first,
             )
 
-        early_banks = ((Y, 1), (Y, 0), (Y, 2), (Z, 0), (Y, 3), (Z, 1))
-        late_banks = ((Z, 2), (Z, 3))
+        early_banks = ((Y, 1), (Y, 0), (Y, 2), (Z, 0), (Y, 3), (Z, 1), (Z, 2))
+        late_banks = ((Z, 3),)
 
         gather_scales(Y)
         gather_scales(Z)
-        move_scales(0, nc.sync)
+        move_scales(0, nc.scalar)
         gather_words(0, Y)
         gather_words(0, Z)
         deal(nc.scalar.copy, 0, 0, 0, HALF)
@@ -143,16 +143,6 @@ def tile_picked_yadain_none_po_kernel(tc, x_words, x_scales, w1, offs, style, ou
         quantise_weights(0, P, 3 * P)
         quantise_weights(0, 3 * P, N)
         move_scales(1, nc.sync)
-        for (l, t), columns in zip(early_banks, (S, S // 2)):
-            nc.tensor.matmul_mx(
-                out=acc[l][t][:, 0:columns],
-                lhsT=w_words[0][:, 0:P].bitcast(FP8X4),
-                lhsT_scale=w_plane[0][:, 0:P],
-                rhs=w_words[0][:, 0:columns].bitcast(FP8X4),
-                rhs_scale=w_plane[0][:, 0:columns],
-                start=True,
-                stop=True,
-            )
         for l, t in early_banks:
             multiply(0, l, t, True)
 

from contextlib import ExitStack

import concourse.mybir as mybir

K, T, S, N = 1024, 2048, 512, 512
EPS = 1e-4
FLOPS = 2 * 2 * K * N * S

F32 = mybir.dt.float32
BF16 = mybir.dt.bfloat16
I32 = mybir.dt.int32
U32 = mybir.dt.uint32
U16 = mybir.dt.uint16
U8 = mybir.dt.uint8
FP8X4 = mybir.dt.float8_e4m3fn_x4
ACT = mybir.ActivationFunctionType
ALU = mybir.AluOpType

P = 128
PACK = 4
PASSES = K // (P * PACK)
QUADS = 4
SCALE_ROWS = 16
PLACE_BYTES = PACK * PACK * 4
HALF = P // 2
TABLE_ROW = P - PASSES * SCALE_ROWS
Y, Z = 0, 1
ROW = (2, 0, 1, 3)

PIECE_1, PIECE_2 = 48, 96
VECTOR_FROM_0 = 80
VECTOR_TO_1 = 122
SCALAR_WEAVES_FROM = 352


def tile_picked_yadain_none_po_kernel(tc, x_words, x_scales, w1, offs, style, out_0, out_1, out_2):
    nc = tc.nc
    with ExitStack() as ctx:
        keep = ctx.enter_context(tc.tile_pool(name="keep", bufs=1))
        stage = ctx.enter_context(tc.tile_pool(name="stage", bufs=1))
        psum = ctx.enter_context(tc.psum_pool(name="psum", bufs=1))

        def sb(name, shape, dtype, align=256):
            return keep.tile(shape, dtype, name=name, align_bytes=align)

        def staged(name, shape, dtype, place):
            return stage.tile(shape, dtype, name=name, align_bytes=1024 if place else 4096, offset=place * PLACE_BYTES)

        lists = [sb("offs_sb", [P, S // 16], U16), sb("style_sb", [P, S // 16], U16)]
        plane_1 = sb("plane1", [P, 2 * S], U8, 1024)
        scale_table = sb("scale_table", [P, T], U8, 2048)
        word_table = [sb("word_table%d" % g, [P, T], I32, 4096) for g in range(PASSES)]
        planes = [sb("plane0", [P, 2 * S], U8, 1024), plane_1]
        picked_scales = sb("picked_scales", [P, 2 * S], U8, 1024)

        nc.vector.memset(scale_table[0:TABLE_ROW, :].bitcast(I32), 0)
        for g in range(PASSES):
            nc.vector.memset(planes[g][:].bitcast(I32), 0)

        ystat = sb("ystat", [P, PACK, 8], F32)
        zstat = sb("zstat", [P, PACK, 8], F32)
        one = sb("one", [P, 1], F32)
        nc.gpsimd.memset(one[:], 1.0)
        nc.scalar.activation(ystat[:, :, 1], one[:].to_broadcast([P, PACK]), ACT.Abs_reciprocal_sqrt, scale=1.0 / EPS ** 2)
        for column, value in ((zstat[:, :, 0], 0.0), (ystat[:, 1:PACK, 0], 1.0 / S), (ystat[:, 1:PACK, 2], -float(S)), (ystat[:, 0, 0:3:2], 1.0)):
            nc.scalar.activation(column, one[:].to_broadcast(list(column.shape)), ACT.Copy, scale=value)

        raw = {}

        def load_words(g):
            nc.sync.dma_start(word_table[g][:], x_words[g].rearrange("p n j -> p (n j)").bitcast(I32))

        def load_weights(g, m0, m1, place):
            rows = w1[g * P * PACK:(g + 1) * P * PACK, :].rearrange("(p j) c -> p j c", j=PACK)
            raw[g, m0] = staged("raw%d_%d" % (g, m0), [P, PACK, PACK * (m1 - m0)], F32, place)
            nc.sync.dma_start(raw[g, m0][:], rows[:, :, PACK * m0:PACK * m1])

        nc.sync.dma_start(scale_table[TABLE_ROW:P, :].bitcast(I32), x_scales.rearrange("g q n -> (g q) n").bitcast(I32))
        nc.sync.dma_start(lists[Y][:], offs)
        nc.sync.dma_start(lists[Z][:], style)
        load_words(0)
        load_weights(0, 0, HALF, PIECE_2 - HALF)
        load_weights(0, HALF, P, PIECE_2)
        load_words(1)

        picked_words = {}
        dealt = [sb("dealt%d" % g, [P, PACK, P, PACK], BF16) for g in range(PASSES)]
        w_words = [sb("w_words%d" % g, [P, N], U32) for g in range(PASSES)]
        w_plane = [sb("w_plane%d" % g, [P, N], U8) for g in range(PASSES)]

        def gather_words(g, l):
            picked_words[g, l] = sb("picked_words%d%d" % (g, l), [P, S], I32)
            nc.vector.tensor_copy(picked_words[g, l][:].bitcast(U32), word_table[g][:].bitcast(U32).indirect(lists[l][:]))

        def gather_scales(l):
            nc.vector.tensor_copy(picked_scales[:, S * l:S * (l + 1)], scale_table[:].indirect(lists[l][:]))

        def move_scales(g, queue):
            for q in range(QUADS):
                src = picked_scales[TABLE_ROW + SCALE_ROWS * g + 4 * q:TABLE_ROW + SCALE_ROWS * g + 4 * q + 4, :]
                queue.dma_start(planes[g][32 * q:32 * q + 4, :].bitcast(I32), src.bitcast(I32))

        def deal(copy, g, piece, m0, m1):
            dst = dealt[g][:, :, m0:m1, :].rearrange("p (u v) m j -> p m u j v", v=2)
            src = raw[g, piece][:, :, PACK * (m0 - piece):PACK * (m1 - piece)].rearrange("p j (m u v) -> p m u j v", u=2, v=2)
            copy(dst, src)

        def quantise_weights(g, c0, c1):
            nc.vector.quantize_mx(
                out=w_words[g][:, c0:c1].bitcast(FP8X4),
                scales=w_plane[g][:, c0:c1],
                in_=dealt[g][:].rearrange("p t m j -> p (t m j)")[:, PACK * c0:PACK * c1],
            )

        acc = [[psum.tile([P, S], F32, name="acc%d%d" % (l, t)) for t in range(PACK)] for l in (Y, Z)]

        def multiply(g, l, t, first):
            nc.tensor.matmul_mx(
                out=acc[l][t][:],
                lhsT=w_words[g][:, P * ROW[t]:P * (ROW[t] + 1)].bitcast(FP8X4),
                lhsT_scale=w_plane[g][:, P * ROW[t]:P * (ROW[t] + 1)],
                rhs=picked_words[g, l][:].bitcast(FP8X4),
                rhs_scale=planes[g][:, S * l:S * (l + 1)],
                start=first,
                stop=not first,
            )

        early_banks = ((Y, 1), (Y, 0), (Y, 2), (Z, 0), (Y, 3), (Z, 1), (Z, 2))
        late_banks = ((Z, 3),)

        gather_scales(Y)
        gather_scales(Z)
        move_scales(0, nc.scalar)
        gather_words(0, Y)
        gather_words(0, Z)
        deal(nc.scalar.copy, 0, 0, 0, HALF)
        deal(nc.scalar.copy, 0, HALF, HALF, VECTOR_FROM_0)
        deal(nc.vector.tensor_copy, 0, HALF, VECTOR_FROM_0, P)
        load_weights(1, 0, PIECE_1, 0)
        load_weights(1, PIECE_1, PIECE_2, PIECE_1)
        load_weights(1, PIECE_2, P, PIECE_2)
        quantise_weights(0, 0, P)
        quantise_weights(0, P, 3 * P)
        quantise_weights(0, 3 * P, N)
        move_scales(1, nc.sync)
        for l, t in early_banks:
            multiply(0, l, t, True)

        gather_words(1, Y)
        gather_words(1, Z)
        deal(nc.scalar.copy, 1, 0, 0, PIECE_1)
        deal(nc.scalar.copy, 1, PIECE_1, PIECE_1, PIECE_2)
        deal(nc.vector.tensor_copy, 1, PIECE_2, PIECE_2, VECTOR_TO_1)
        deal(nc.scalar.copy, 1, PIECE_2, VECTOR_TO_1, P)
        for t in (1, 0):
            quantise_weights(1, P * ROW[t], P * ROW[t] + HALF)
        for t in (1, 0):
            quantise_weights(1, P * ROW[t] + HALF, P * (ROW[t] + 1))
        for t in (2, 3):
            quantise_weights(1, P * ROW[t], P * (ROW[t] + 1))
        for l, t in early_banks:
            multiply(1, l, t, False)
        for l, t in late_banks:
            multiply(1, l, t, True)
            multiply(0, l, t, False)

        y_copy = {t: sb("y_copy%d" % t, [P, S], F32) for t in range(1, PACK)}
        squares = sb("squares", [P, PACK, S], BF16)
        sum_sq = sb("sum_sq", [P, PACK], F32)
        tuples = [[sb("tuples%d%d" % (l, t), [P, 6], F32) for t in range(PACK)] for l in (Y, Z)]
        prod = sb("prod", [P, PACK, 4], F32)
        root = [sb("root%d" % t, [P, 1], F32) for t in range(PACK)]
        gain = [sb("gain%d" % t, [P, 2], F32) for t in range(PACK)]
        shift_0 = sb("shift_0", [P, 1], F32)
        res = sb("res", [P, PACK, S], F32, 4096)
        out_rows = out_0.rearrange("(p t) c -> p t c", t=PACK)

        def first_read(t):
            nc.scalar.activation(y_copy[t][:], acc[Y][t][:], ACT.Copy, scale=-1.0 / S, accum_out=ystat[:, t, 3:4])

        def second_read(t):
            nc.scalar.activation(squares[:, t, :], acc[Y][t][:], ACT.Square, bias=ystat[:, t, 3:4], accum_out=sum_sq[:, t:t + 1])

        def bn_read(l, t):
            nc.vector.bn_stats(tuples[l][t][:], acc[l][t][:])

        def bn_join(l, t):
            nc.vector.bn_aggr(zstat[:, t, 1:3] if l == Z else ystat[:, t, 3:5], tuples[l][t][:])

        def products(t0, t1):
            var_z = zstat[:, t0:t1, 2:3].to_broadcast([P, t1 - t0, 4])
            nc.vector.scalar_tensor_tensor(prod[:, t0:t1, :], var_z, EPS, ystat[:, t0:t1, 0:4], ALU.add, ALU.mult)

        def inverse_root(t):
            spread_y = sum_sq[:, t:t + 1] if t else ystat[:, t, 4:5]
            nc.scalar.activation(root[t][:], spread_y, ACT.Abs_reciprocal_sqrt, scale=prod[:, t, 0:1], bias=prod[:, t, 1:2])

        def gains(t):
            nc.vector.scalar_tensor_tensor(gain[t][:], prod[:, t, 2:4], root[t][:], zstat[:, t, 0:2], ALU.mult, ALU.add if t else ALU.subtract)

        def affine(t):
            nc.vector.tensor_scalar(res[:, ROW[t], :], y_copy[t][:], gain[t][:, 0:1], gain[t][:, 1:2], ALU.mult, ALU.add)

        def store(tiles):
            nc.sync.dma_start(out_rows[:, tiles, :], res[:, tiles, :])

        first_read(1)
        first_read(2)
        second_read(1)
        first_read(3)
        second_read(2)
        second_read(3)
        bn_read(Y, 0)
        bn_read(Z, 0)
        bn_join(Y, 0)
        bn_read(Z, 1)
        bn_join(Z, 0)
        bn_read(Z, 2)
        bn_join(Z, 1)
        products(0, 2)
        inverse_root(1)
        inverse_root(0)
        bn_read(Z, 3)
        bn_join(Z, 2)
        gains(1)
        products(2, 3)
        bn_join(Z, 3)
        inverse_root(2)
        gains(0)
        products(3, PACK)
        inverse_root(3)
        gains(2)
        affine(1)
        store(slice(0, 1))
        gains(3)
        nc.scalar.activation(shift_0[:], gain[0][:, 1:2], ACT.Copy, scale=-1.0)
        nc.scalar.activation(res[:, ROW[0], :], acc[Y][0][:], ACT.Identity, scale=gain[0][:, 0:1], bias=shift_0[:])
        affine(2)
        store(slice(1, 2))
        affine(3)
        store(slice(2, PACK))

        woven = [sb("woven%d" % h, [P, S // 2, PACK], BF16) for h in range(2)]
        out_words = sb("out_words", [P, S], U32, 2048)
        out_plane = sb("out_plane", [P, S], U8, 512)
        words_dram = out_1[0].rearrange("p n t -> p (n t)").bitcast(I32)

        def weave(copy, h, c0, c1):
            dst = woven[h][:, c0 - h * S // 2:c1 - h * S // 2, :].rearrange("p (c i) t -> p c t i", i=4)
            src = res[:, :, c0:c1].rearrange("p t (c i) -> p c t i", i=4)
            copy(dst, src)

        weave(nc.vector.tensor_copy, 0, 0, S // 2)
        weave(nc.scalar.copy, 1, SCALAR_WEAVES_FROM, S)
        weave(nc.vector.tensor_copy, 1, S // 2, SCALAR_WEAVES_FROM)
        for h in range(2):
            cols = slice(h * S // 2, (h + 1) * S // 2)
            nc.vector.quantize_mx(out=out_words[:, cols].bitcast(FP8X4), scales=out_plane[:, cols], in_=woven[h][:].rearrange("p c t -> p (c t)"))
        nc.sync.dma_start(words_dram, out_words[:].bitcast(I32))
        for q in range(QUADS):
            queue = nc.scalar if q % 2 else nc.sync
            queue.dma_start(out_2[0, 4 * q:4 * q + 4, :].bitcast(I32), out_plane[32 * q:32 * q + 4, :].bitcast(I32))
